import numpy as np
import ml_dtypes


def mxq(x, axis, fmt="e4m3"):
    dtype, down = {"e4m3": (ml_dtypes.float8_e4m3fn, 7), "e5m2": (ml_dtypes.float8_e5m2, 14)}[fmt]
    v = np.moveaxis(np.asarray(x, np.float32).astype(ml_dtypes.bfloat16).astype(np.float64), axis, -1)
    blocks = v.reshape(v.shape[:-1] + (-1, 32))
    amax = np.abs(blocks).max(-1, keepdims=True)
    byte = np.maximum(np.where(amax > 0, np.frexp(amax)[1] - 1 + 127, 0) - down, 1)
    scale = np.exp2(byte - 127.0)
    codes = (blocks / scale).astype(np.float32).astype(dtype).astype(np.float64)
    return np.moveaxis((codes * scale).reshape(v.shape), -1, axis)


WIDE = False


def mx_kscale(k):
    if not WIDE:
        return np.ones(k)
    levels = np.array([30, -30])
    if k % 512:
        return np.exp2(np.random.permutation(np.resize(levels, k // 32))).repeat(32)
    a = np.empty((k // 512, 16))
    for p in range(k // 512):
        a[p, :8] = np.random.permutation(np.resize(levels, 8))
        for g in range(8):
            far = levels[np.abs(levels - a[p, g]) >= 10]
            a[p, g + 8] = far[np.random.randint(len(far))]
    return np.exp2(a.ravel()).repeat(32)


BF16 = ml_dtypes.bfloat16


def bf(x):
    return np.asarray(x, np.float32).astype(BF16)


def f64(x):
    return np.asarray(x).astype(np.float64)


M, T, L = 1024, 1024, 1536


def setup_inputs():
    s = mx_kscale(T)
    t = mx_kscale(L)
    thrust = np.exp(0.6 * np.random.standard_normal((M, T)))
    area = np.random.uniform(0.5, 2.0, T)
    kern = np.square(np.random.standard_normal((T, T))) / (20.0 * T)
    outer = np.random.exponential(1.0, (M, L))
    okern = np.random.standard_normal((L, T)) ** 4 / (24.0 * L)
    inflow = np.random.uniform(1.3, 1.7, M)
    return {"thrust": bf(thrust),
            "area": bf(area * s),
            "kern": bf(kern / s[:, None]),
            "outer": bf(outer * t),
            "okern": bf(okern / t[:, None]),
            "inflow": bf(inflow)}


def reference(thrust, area, kern, outer, okern, inflow):
    a = np.square(f64(thrust)) * f64(area)
    own = mxq(a, 1, "e5m2") @ mxq(f64(kern), 0, "e4m3")
    ext = mxq(f64(outer), 1, "e4m3") @ mxq(f64(okern), 0, "e4m3")
    d2 = own + ext
    speed = f64(inflow)[:, None] - np.sqrt(d2)
    power = speed ** 3
    return speed, power

@@ -1,0 +1,356 @@
+from contextlib import ExitStack
+
+import concourse.mybir as mybir
+from concourse.masks import make_identity
+
+M, T, L, N = 1024, 1024, 1536, 1024
+FLOPS = 2 * M * N * (T + L)
+
+F32 = mybir.dt.float32
+BF16 = mybir.dt.bfloat16
+U32 = mybir.dt.uint32
+U8 = mybir.dt.uint8
+E4M3 = mybir.dt.float8_e4m3fn_x4
+E5M2 = mybir.dt.float8_e5m2_x4
+ACT = mybir.ActivationFunctionType
+ALU = mybir.AluOpType
+
+P = 128
+KP = 512
+GT = T // KP
+GL = L // KP
+NW = GT + GL
+ROWS = M // P
+PAIRS = ROWS // 2
+H = 512
+Q = 256
+
+
+def tile_wind_farm_wakes_s2_kernel(tc, thrust, area, kern, outer, okern, inflow, speed, power):
+    nc = tc.nc
+    with ExitStack() as ctx:
+        keep = ctx.enter_context(tc.tile_pool(name="keep", bufs=1))
+        work = ctx.enter_context(tc.tile_pool(name="work", bufs=2))
+        turn = ctx.enter_context(tc.psum_pool(name="turn", bufs=4))
+        sums = ctx.enter_context(tc.psum_pool(name="sums", bufs=4))
+
+        area_b = keep.tile([P, GT, 4], BF16, name="area_b")
+        inflow_b = keep.tile([P, ROWS], BF16, name="inflow_b")
+        nc.scalar.dma_start(out=area_b[:], in_=area.rearrange("(g p j) -> p g j", g=GT, j=4))
+        nc.scalar.dma_start(out=inflow_b[:], in_=inflow.rearrange("(p t) -> p t", t=ROWS))
+        ident = keep.tile([P, P], F32, name="ident")
+        make_identity(nc, ident[:])
+        dummy = keep.tile([P, 1], F32, name="dummy")
+        nc.gpsimd.memset(dummy[:], 1.0)
+        nc.scalar.activation(out=dummy[:], in_=dummy[:], func=ACT.Sqrt)
+        inflow_f = keep.tile([P, ROWS], F32, name="inflow_f")
+
+        w_hbm = [kern[g * KP:(g + 1) * KP, :] for g in range(GT)] + [okern[g * KP:(g + 1) * KP, :] for g in range(GL)]
+        w_raw = {}
+        t_raw = {}
+        o_raw = {}
+
+        def load_w(w, c0, width):
+            raw = keep.tile([P, 4, width], BF16, name="w_raw_%d_%d" % (w, c0), align_bytes=64)
+            nc.sync.dma_start(out=raw[:], in_=w_hbm[w].rearrange("(p j) n -> p j n", j=4)[:, :, c0:c0 + width])
+            for c in range(c0, c0 + width, Q):
+                w_raw[w, c] = raw[:, :, c - c0:]
+
+        def load_t(i):
+            t_raw[i] = work.tile([P, 2, T], BF16, name="t_raw", bufs=3, align_bytes=64)
+            nc.sync.dma_start(out=t_raw[i][:], in_=thrust.rearrange("(p t) k -> p t k", t=ROWS)[:, 2 * i:2 * i + 2, :])
+
+        def load_o(i):
+            o_raw[i] = work.tile([P, 2, L], BF16, name="o_raw", bufs=3, align_bytes=64)
+            nc.sync.dma_start(out=o_raw[i][:], in_=outer.rearrange("(p t) k -> p t k", t=ROWS)[:, 2 * i:2 * i + 2, :])
+
+        w_codes = [keep.tile([P, N], U32, name="w_codes_%d" % w, align_bytes=64) for w in range(NW)]
+        w_scales = [keep.tile([P, N], U8, name="w_scales_%d" % w, align_bytes=64) for w in range(NW)]
+        w_lay = {}
+
+        def lay(w, h, copy, c0=0, c1=H):
+            if (w, 0) not in w_lay:
+                w_lay[w, 0] = work.tile([P, N, 4], BF16, name="w_lay", bufs=3, align_bytes=64)
+            copy(
+                out=w_lay[w, 0][:, h * H + c0:h * H + c1].rearrange("p (c i) j -> p c j i", i=4),
+                in_=w_raw[w, h * H + c0][:, :, 0:c1 - c0].rearrange("p j (c i) -> p c j i", i=4),
+            )
+
+        def quant_w(w, h):
+            cols = slice(h * H, (h + 1) * H)
+            nc.vector.quantize_mx(
+                out=w_codes[w][:, cols].bitcast(E4M3),
+                scales=w_scales[w][:, cols],
+                in_=w_lay[w, 0][:, cols].rearrange("p c j -> p (c j)"),
+            )
+
+        x_codes = {}
+        x_scales = {}
+        for i in range(PAIRS):
+            x_codes[i] = keep.tile([P, NW, 2 * P], U32, name="x_codes_%d" % i, align_bytes=64)
+            x_scales[i] = keep.tile([P, NW, 2 * P], U8, name="x_scales_%d" % i, align_bytes=64)
+
+        banks = {}
+
+        def turn_x(raw, g):
+            bank = turn.tile([P, 2, 2 * P], F32, name="bank")
+            words = raw[:].bitcast(F32)
+            for mt in range(2):
+                for u in range(2):
+                    nc.tensor.transpose(
+                        bank[:, u, mt * P:(mt + 1) * P],
+                        words[:, mt, 256 * g + u:256 * (g + 1):2],
+                        ident[:],
+                    )
+            return bank
+
+        def turn_t(i, g):
+            banks["t", i, g] = turn_x(t_raw[i], g)
+
+        def turn_o(i, g):
+            banks["o", i, g] = turn_x(o_raw[i], g)
+
+        t_sq = {}
+        t_a = {}
+        o_lay = {}
+
+
+        def square_t(i, g):
+            if i not in t_sq:
+                t_sq[i] = work.tile([P, GT, 2 * P, 4], F32, name="t_sq", bufs=2, align_bytes=64)
+            nc.scalar.activation(
+                out=t_sq[i][:, g].rearrange("p c (u e) -> p c u e", e=2),
+                in_=banks["t", i, g][:].bitcast(BF16).rearrange("p u (c e) -> p c u e", e=2),
+                func=ACT.Square,
+            )
+
+        def area_t(i, g):
+            if i not in t_a:
+                t_a[i] = work.tile([P, GT, 2 * P, 4], BF16, name="t_a", bufs=2, align_bytes=64)
+            nc.vector.tensor_tensor(
+                out=t_a[i][:, g],
+                in0=t_sq[i][:, g],
+                in1=area_b[:, g, :].unsqueeze(1).to_broadcast([P, 2 * P, 4]),
+                op=ALU.mult,
+            )
+
+        def quant_w2(w):
+            nc.vector.quantize_mx(
+                out=w_codes[w][:].bitcast(E4M3),
+                scales=w_scales[w][:],
+                in_=w_lay[w, 0][:].rearrange("p c j -> p (c j)"),
+            )
+
+        def quant_t(i):
+            nc.vector.quantize_mx(
+                out=x_codes[i][:, 0:GT, :].rearrange("p g c -> p (g c)").bitcast(E5M2),
+                scales=x_scales[i][:, 0:GT, :].rearrange("p g c -> p (g c)"),
+                in_=t_a[i][:].rearrange("p g c j -> p (g c j)"),
+            )
+
+        def lay_o(i, g, copy):
+            if i not in o_lay:
+                o_lay[i] = work.tile([P, GL, 2 * P, 2], F32, name="o_lay", bufs=2, align_bytes=64)
+            copy(out=o_lay[i][:, g], in_=banks["o", i, g][:].rearrange("p u c -> p c u"))
+
+        def quant_o(i, part):
+            src = o_lay[i][:].rearrange("p g c u -> p g (c u)").bitcast(BF16)
+            for g0, g1 in (((0, 2), (2, 3))[part],):
+                nc.vector.quantize_mx(
+                    out=x_codes[i][:, GT + g0:GT + g1, :].rearrange("p g c -> p (g c)").bitcast(E4M3),
+                    scales=x_scales[i][:, GT + g0:GT + g1, :].rearrange("p g c -> p (g c)"),
+                    in_=src[:, g0:g1, :].rearrange("p g c -> p (g c)"),
+                )
+
+        acc = {}
+
+        def mx(i, mt, h, passes):
+            if (i, mt, h) not in acc:
+                acc[i, mt, h] = sums.tile([P, H], F32, name="acc")
+            rows = slice(mt * P, (mt + 1) * P)
+            cols = slice(h * H, (h + 1) * H)
+            for w in passes:
+                nc.tensor.matmul_mx(
+                    out=acc[i, mt, h][:],
+                    lhsT=x_codes[i][:, w, rows].bitcast(E5M2 if w < GT else E4M3),
+                    lhsT_scale=x_scales[i][:, w, rows],
+                    rhs=w_codes[w][:, cols].bitcast(E4M3),
+                    rhs_scale=w_scales[w][:, cols],
+                    start=(w == 0),
+                    stop=(w == NW - 1),
+                )
+
+        def mx_all(i, passes):
+            for mt in range(2):
+                for h in range(2):
+                    mx(i, mt, h, passes)
+
+        root = {}
+        vel = {}
+        vel2 = {}
+        pw = {}
+
+        def root_d2(i, mt, h):
+            if (i, mt) not in root:
+                root[i, mt] = work.tile([P, N], F32, name="root", bufs=3)
+            nc.scalar.activation(out=root[i, mt][:, h * H:(h + 1) * H], in_=acc[i, mt, h][:], func=ACT.Sqrt)
+
+        def square_v(i, mt, c0=0, c1=N):
+            r = 2 * i + mt
+            if (i, mt) not in vel2:
+                vel2[i, mt] = work.tile([P, N], F32, name="vel2", bufs=2)
+            nc.scalar.activation(
+                out=vel2[i, mt][:, c0:c1], in_=root[i, mt][:, c0:c1], func=ACT.Square, scale=-1.0, bias=inflow_f[:, r:r + 1]
+            )
+
+        def speed_v(i, mt, c0=0, c1=N):
+            r = 2 * i + mt
+            if (i, mt) not in vel:
+                vel[i, mt] = work.tile([P, N], F32, name="vel", bufs=4)
+            nc.vector.tensor_scalar(
+                out=vel[i, mt][:, c0:c1], in0=root[i, mt][:, c0:c1], scalar1=-1.0, scalar2=inflow_f[:, r:r + 1],
+                op0=ALU.mult, op1=ALU.add,
+            )
+            nc.sync.dma_start(out=speed.rearrange("(p t) n -> p t n", t=ROWS)[:, r, c0:c1], in_=vel[i, mt][:, c0:c1])
+
+        def square_dve(i, mt, c0, c1):
+            nc.vector.tensor_tensor(
+                out=vel2[i, mt][:, c0:c1], in0=vel[i, mt][:, c0:c1], in1=vel[i, mt][:, c0:c1], op=ALU.mult
+            )
+
+        def power_v(i, mt, c0=0, c1=N):
+            r = 2 * i + mt
+            if (i, mt) not in pw:
+                pw[i, mt] = work.tile([P, N], F32, name="pw", bufs=4)
+            nc.vector.tensor_tensor(
+                out=pw[i, mt][:, c0:c1], in0=vel2[i, mt][:, c0:c1], in1=vel[i, mt][:, c0:c1], op=ALU.mult
+            )
+            nc.sync.dma_start(out=power.rearrange("(p t) n -> p t n", t=ROWS)[:, r, c0:c1], in_=pw[i, mt][:, c0:c1])
+
+        act_copy = nc.scalar.copy
+        dve_copy = nc.vector.tensor_copy
+
+        load_w(0, 0, H)
+        load_t(0)
+        load_w(0, H, H)
+        load_o(0)
+        load_w(1, 0, N)
+        load_t(1)
+        load_w(2, 0, N)
+        load_w(3, 0, N)
+        load_o(1)
+        load_w(4, 0, N)
+        load_t(2)
+        load_o(2)
+
+        lay(0, 0, act_copy, 0, Q)
+        lay(0, 0, dve_copy, Q, H)
+        turn_t(0, 0)
+        turn_t(0, 1)
+        square_t(0, 0)
+        square_t(0, 1)
+        quant_w(0, 0)
+        lay(0, 1, dve_copy)
+        turn_o(0, 0)
+        turn_o(0, 1)
+        turn_o(0, 2)
+        lay_o(0, 0, act_copy)
+        lay_o(0, 1, act_copy)
+        area_t(0, 0)
+        area_t(0, 1)
+        lay_o(0, 2, act_copy)
+        quant_w(0, 1)
+        lay(1, 1, act_copy)
+        lay(1, 0, dve_copy)
+        turn_t(1, 0)
+        turn_t(1, 1)
+        square_t(1, 0)
+        quant_t(0)
+        quant_o(0, 0)
+        quant_o(0, 1)
+        quant_w2(1)
+        for w in range(2):
+            mx_all(0, [w])
+
+        lay(2, 0, dve_copy)
+        lay(2, 1, act_copy)
+        square_t(1, 1)
+        turn_o(1, 0)
+        turn_o(1, 1)
+        turn_o(1, 2)
+        load_t(3)
+        load_o(3)
+        turn_t(2, 0)
+        lay(3, 0, dve_copy)
+        quant_w2(2)
+        lay(3, 1, act_copy)
+        lay_o(1, 0, act_copy)
+        lay_o(1, 1, act_copy)
+        lay_o(1, 2, dve_copy)
+        area_t(1, 0)
+        lay(4, 0, dve_copy)
+        quant_w2(3)
+        turn_t(2, 1)
+        turn_o(2, 0)
+        turn_o(2, 1)
+        for w in range(2, 4):
+            mx_all(0, [w])
+
+        lay(4, 1, act_copy)
+        square_t(2, 0)
+        square_t(2, 1)
+        turn_t(3, 0)
+        turn_t(3, 1)
+        turn_o(2, 2)
+        area_t(1, 1)
+        nc.vector.tensor_copy(out=inflow_f[:], in_=inflow_b[:])
+        quant_o(1, 0)
+        quant_o(1, 1)
+        quant_w2(4)
+        lay_o(2, 0, act_copy)
+        lay_o(2, 1, act_copy)
+        square_t(3, 0)
+        quant_t(1)
+        mx_all(0, [4])
+        area_t(2, 0)
+
+        groups = [(i, mt, h) for i in range(PAIRS) for mt in range(2) for h in range(2)]
+        for r in range(ROWS):
+            i, mt = divmod(r, 2)
+            last = r == ROWS - 1
+            for h in range(2):
+                root_d2(i, mt, h)
+                k = 2 * r + h + 4
+                if k < 2 * ROWS:
+                    mx(*groups[k], range(NW))
+                if last:
+                    speed_v(i, mt, h * H, (h + 1) * H)
+                    square_v(i, mt, h * H, (h + 1) * H)
+                    power_v(i, mt, h * H, (h + 1) * H)
+            if r == 0:
+                lay_o(2, 2, act_copy)
+            if r == 1:
+                square_t(3, 1)
+                lay_o(3, 0, act_copy)
+            if not last:
+                speed_v(i, mt)
+                square_v(i, mt)
+            if r == 0:
+                area_t(2, 1)
+                turn_o(3, 0)
+                turn_o(3, 1)
+                turn_o(3, 2)
+                quant_t(2)
+                quant_o(2, 0)
+                quant_o(2, 1)
+            if r == 1:
+                lay_o(3, 1, act_copy)
+                area_t(3, 0)
+                area_t(3, 1)
+            if r == 2:
+                lay_o(3, 2, act_copy)
+                quant_t(3)
+                quant_o(3, 0)
+                quant_o(3, 1)
+            if not last:
+                power_v(i, mt)

@@ -24,6 +24,7 @@ ROWS = M // P
 PAIRS = ROWS // 2
 H = 512
 Q = 256
+W4_SPLIT = 736
 
 
 def tile_wind_farm_wakes_s2_kernel(tc, thrust, area, kern, outer, okern, inflow, speed, power):
@@ -31,326 +32,316 @@ def tile_wind_farm_wakes_s2_kernel(tc, thrust, area, kern, outer, okern, inflow,
     with ExitStack() as ctx:
         keep = ctx.enter_context(tc.tile_pool(name="keep", bufs=1))
         work = ctx.enter_context(tc.tile_pool(name="work", bufs=2))
-        turn = ctx.enter_context(tc.psum_pool(name="turn", bufs=4))
-        sums = ctx.enter_context(tc.psum_pool(name="sums", bufs=4))
+        psum = ctx.enter_context(tc.psum_pool(name="psum", bufs=1))
+        ctx.enter_context(tc.manual_schedule())
 
         area_b = keep.tile([P, GT, 4], BF16, name="area_b")
-        inflow_b = keep.tile([P, ROWS], BF16, name="inflow_b")
+        inflow_f = keep.tile([P, ROWS], BF16, name="inflow_f")
         nc.scalar.dma_start(out=area_b[:], in_=area.rearrange("(g p j) -> p g j", g=GT, j=4))
-        nc.scalar.dma_start(out=inflow_b[:], in_=inflow.rearrange("(p t) -> p t", t=ROWS))
-        ident = keep.tile([P, P], F32, name="ident")
-        make_identity(nc, ident[:])
         dummy = keep.tile([P, 1], F32, name="dummy")
         nc.gpsimd.memset(dummy[:], 1.0)
         nc.scalar.activation(out=dummy[:], in_=dummy[:], func=ACT.Sqrt)
-        inflow_f = keep.tile([P, ROWS], F32, name="inflow_f")
+        ident = keep.tile([P, P], F32, name="ident")
+        make_identity(nc, ident[:])
 
         w_hbm = [kern[g * KP:(g + 1) * KP, :] for g in range(GT)] + [okern[g * KP:(g + 1) * KP, :] for g in range(GL)]
+        thrust_rows = thrust.rearrange("(p t) k -> p t k", t=ROWS)
+        outer_rows = outer.rearrange("(p t) k -> p t k", t=ROWS)
+        speed_rows = speed.rearrange("(p t) n -> p t n", t=ROWS)
+        power_rows = power.rearrange("(p t) n -> p t n", t=ROWS)
         w_raw = {}
         t_raw = {}
         o_raw = {}
 
-        def load_w(w, c0, width):
-            raw = keep.tile([P, 4, width], BF16, name="w_raw_%d_%d" % (w, c0), align_bytes=64)
-            nc.sync.dma_start(out=raw[:], in_=w_hbm[w].rearrange("(p j) n -> p j n", j=4)[:, :, c0:c0 + width])
-            for c in range(c0, c0 + width, Q):
+        def load_w(w, c0, c1):
+            raw = keep.tile([P, 4, c1 - c0], BF16, name="w_raw_%d_%d" % (w, c0), align_bytes=64)
+            nc.sync.dma_start(out=raw[:], in_=w_hbm[w].rearrange("(p j) n -> p j n", j=4)[:, :, c0:c1])
+            for c in range(c0, c1, 32):
                 w_raw[w, c] = raw[:, :, c - c0:]
 
-        def load_t(i):
-            t_raw[i] = work.tile([P, 2, T], BF16, name="t_raw", bufs=3, align_bytes=64)
-            nc.sync.dma_start(out=t_raw[i][:], in_=thrust.rearrange("(p t) k -> p t k", t=ROWS)[:, 2 * i:2 * i + 2, :])
+        def load_t(r0, r1):
+            raw = keep.tile([P, r1 - r0, T], BF16, name="t_raw_%d" % r0, align_bytes=64)
+            nc.sync.dma_start(out=raw[:], in_=thrust_rows[:, r0:r1, :])
+            for r in range(r0, r1):
+                t_raw[r] = raw[:, r - r0, :]
 
-        def load_o(i):
-            o_raw[i] = work.tile([P, 2, L], BF16, name="o_raw", bufs=3, align_bytes=64)
-            nc.sync.dma_start(out=o_raw[i][:], in_=outer.rearrange("(p t) k -> p t k", t=ROWS)[:, 2 * i:2 * i + 2, :])
+        def load_o(r0, r1):
+            raw = keep.tile([P, r1 - r0, L], BF16, name="o_raw_%d" % r0, align_bytes=64)
+            nc.sync.dma_start(out=raw[:], in_=outer_rows[:, r0:r1, :])
+            for r in range(r0, r1):
+                o_raw[r] = raw[:, r - r0, :]
 
         w_codes = [keep.tile([P, N], U32, name="w_codes_%d" % w, align_bytes=64) for w in range(NW)]
         w_scales = [keep.tile([P, N], U8, name="w_scales_%d" % w, align_bytes=64) for w in range(NW)]
         w_lay = {}
 
-        def lay(w, h, copy, c0=0, c1=H):
-            if (w, 0) not in w_lay:
-                w_lay[w, 0] = work.tile([P, N, 4], BF16, name="w_lay", bufs=3, align_bytes=64)
+        def lay_w(w, c0, c1, copy):
+            h = c0 // H
+            if (w, h) not in w_lay:
+                w_lay[w, h] = work.tile([P, H, 4], BF16, name="w_lay", bufs=4, align_bytes=64)
             copy(
-                out=w_lay[w, 0][:, h * H + c0:h * H + c1].rearrange("p (c i) j -> p c j i", i=4),
-                in_=w_raw[w, h * H + c0][:, :, 0:c1 - c0].rearrange("p j (c i) -> p c j i", i=4),
+                out=w_lay[w, h][:, c0 - h * H:c1 - h * H].rearrange("p (c i) j -> p c j i", i=4),
+                in_=w_raw[w, c0][:, :, 0:c1 - c0].rearrange("p j (c i) -> p c j i", i=4),
             )
 
-        def quant_w(w, h):
-            cols = slice(h * H, (h + 1) * H)
+        def quant_w(w, c0, c1):
             nc.vector.quantize_mx(
-                out=w_codes[w][:, cols].bitcast(E4M3),
-                scales=w_scales[w][:, cols],
-                in_=w_lay[w, 0][:, cols].rearrange("p c j -> p (c j)"),
+                out=w_codes[w][:, c0:c1].bitcast(E4M3),
+                scales=w_scales[w][:, c0:c1],
+                in_=w_lay[w, c0 // H][:, c0 % H:c0 % H + c1 - c0].rearrange("p c j -> p (c j)"),
             )
 
-        x_codes = {}
-        x_scales = {}
-        for i in range(PAIRS):
-            x_codes[i] = keep.tile([P, NW, 2 * P], U32, name="x_codes_%d" % i, align_bytes=64)
-            x_scales[i] = keep.tile([P, NW, 2 * P], U8, name="x_scales_%d" % i, align_bytes=64)
+        a_codes = keep.tile([P, ROWS * GT * P], U32, name="a_codes", align_bytes=64)
+        a_scales = keep.tile([P, ROWS * GT * P], U8, name="a_scales", align_bytes=64)
+        o_codes = keep.tile([P, ROWS * GL * P], U32, name="o_codes", align_bytes=64)
+        o_scales = keep.tile([P, ROWS * GL * P], U8, name="o_scales", align_bytes=64)
 
         banks = {}
+        held = {}
+        empty = list(range(8))
 
-        def turn_x(raw, g):
-            bank = turn.tile([P, 2, 2 * P], F32, name="bank")
-            words = raw[:].bitcast(F32)
-            for mt in range(2):
+        def take_bank(key, shape):
+            held[key] = empty.pop(0)
+            banks[key] = psum.tile(shape, F32, name="bank_%d" % held[key])
+            return banks[key]
+
+        def give_bank(key):
+            empty.append(held.pop(key))
+
+        def turn_units(key, units):
+            bank = take_bank(key, [P, 2, 2 * P])
+            for s, (raw, g) in enumerate(units):
+                words = raw.bitcast(F32)
                 for u in range(2):
-                    nc.tensor.transpose(
-                        bank[:, u, mt * P:(mt + 1) * P],
-                        words[:, mt, 256 * g + u:256 * (g + 1):2],
-                        ident[:],
-                    )
-            return bank
+                    nc.tensor.transpose(bank[:, u, s * P:(s + 1) * P], words[:, 256 * g + u:256 * (g + 1):2], ident[:])
 
-        def turn_t(i, g):
-            banks["t", i, g] = turn_x(t_raw[i], g)
+        def turn_t(r):
+            turn_units(("t", r), [(t_raw[r], g) for g in range(GT)])
 
-        def turn_o(i, g):
-            banks["o", i, g] = turn_x(o_raw[i], g)
+        def turn_o(b):
+            turn_units(("o", b), [(o_raw[s // GL], s % GL) for s in (2 * b, 2 * b + 1)])
 
         t_sq = {}
         t_a = {}
         o_lay = {}
 
-
-        def square_t(i, g):
-            if i not in t_sq:
-                t_sq[i] = work.tile([P, GT, 2 * P, 4], F32, name="t_sq", bufs=2, align_bytes=64)
+        def square_t(r):
+            t_sq[r] = work.tile([P, 2 * P, 4], F32, name="t_sq", bufs=3, align_bytes=64)
             nc.scalar.activation(
-                out=t_sq[i][:, g].rearrange("p c (u e) -> p c u e", e=2),
-                in_=banks["t", i, g][:].bitcast(BF16).rearrange("p u (c e) -> p c u e", e=2),
+                out=t_sq[r][:].rearrange("p c (u e) -> p c u e", e=2),
+                in_=banks["t", r][:].bitcast(BF16).rearrange("p u (c e) -> p c u e", e=2),
                 func=ACT.Square,
             )
+            give_bank(("t", r))
 
-        def area_t(i, g):
-            if i not in t_a:
-                t_a[i] = work.tile([P, GT, 2 * P, 4], BF16, name="t_a", bufs=2, align_bytes=64)
+        def area_t(r):
+            if r % 2 == 0:
+                t_a[r // 2] = work.tile([P, 2, GT, P, 4], BF16, name="t_a", bufs=2, align_bytes=64)
             nc.vector.tensor_tensor(
-                out=t_a[i][:, g],
-                in0=t_sq[i][:, g],
-                in1=area_b[:, g, :].unsqueeze(1).to_broadcast([P, 2 * P, 4]),
+                out=t_a[r // 2][:, r % 2],
+                in0=t_sq[r][:].rearrange("p (g c) j -> p g c j", g=GT),
+                in1=area_b[:].unsqueeze(2).to_broadcast([P, GT, P, 4]),
                 op=ALU.mult,
             )
 
-        def quant_w2(w):
+        def quant_t(r0, r1):
+            cols = slice(r0 * GT * P, r1 * GT * P)
             nc.vector.quantize_mx(
-                out=w_codes[w][:].bitcast(E4M3),
-                scales=w_scales[w][:],
-                in_=w_lay[w, 0][:].rearrange("p c j -> p (c j)"),
+                out=a_codes[:, cols].bitcast(E5M2),
+                scales=a_scales[:, cols],
+                in_=t_a[r0 // 2][:, r0 % 2:r0 % 2 + r1 - r0].rearrange("p r g c j -> p (r g c j)"),
             )
 
-        def quant_t(i):
-            nc.vector.quantize_mx(
-                out=x_codes[i][:, 0:GT, :].rearrange("p g c -> p (g c)").bitcast(E5M2),
-                scales=x_scales[i][:, 0:GT, :].rearrange("p g c -> p (g c)"),
-                in_=t_a[i][:].rearrange("p g c j -> p (g c j)"),
-            )
+        def lay_o(b, copy):
+            if b % GL == 0:
+                o_lay[b // GL] = work.tile([P, GL, 2 * P, 2], F32, name="o_lay", bufs=2, align_bytes=64)
+            copy(out=o_lay[b // GL][:, b % GL], in_=banks["o", b][:].rearrange("p u c -> p c u"))
+            give_bank(("o", b))
 
-        def lay_o(i, g, copy):
-            if i not in o_lay:
-                o_lay[i] = work.tile([P, GL, 2 * P, 2], F32, name="o_lay", bufs=2, align_bytes=64)
-            copy(out=o_lay[i][:, g], in_=banks["o", i, g][:].rearrange("p u c -> p c u"))
+        def quant_o(b0, b1):
+            cols = slice(b0 * 2 * P, b1 * 2 * P)
+            src = o_lay[b0 // GL][:, b0 % GL:b0 % GL + b1 - b0].rearrange("p g c u -> p (g c u)").bitcast(BF16)
+            nc.vector.quantize_mx(out=o_codes[:, cols].bitcast(E4M3), scales=o_scales[:, cols], in_=src)
 
-        def quant_o(i, part):
-            src = o_lay[i][:].rearrange("p g c u -> p g (c u)").bitcast(BF16)
-            for g0, g1 in (((0, 2), (2, 3))[part],):
-                nc.vector.quantize_mx(
-                    out=x_codes[i][:, GT + g0:GT + g1, :].rearrange("p g c -> p (g c)").bitcast(E4M3),
-                    scales=x_scales[i][:, GT + g0:GT + g1, :].rearrange("p g c -> p (g c)"),
-                    in_=src[:, g0:g1, :].rearrange("p g c -> p (g c)"),
-                )
-
-        acc = {}
-
-        def mx(i, mt, h, passes):
-            if (i, mt, h) not in acc:
-                acc[i, mt, h] = sums.tile([P, H], F32, name="acc")
-            rows = slice(mt * P, (mt + 1) * P)
+        def mx(r, h, passes):
+            if (r, h) not in banks:
+                take_bank((r, h), [P, H])
             cols = slice(h * H, (h + 1) * H)
             for w in passes:
+                if w < GT:
+                    rows = slice((r * GT + w) * P, (r * GT + w + 1) * P)
+                    codes, scales = a_codes[:, rows].bitcast(E5M2), a_scales[:, rows]
+                else:
+                    rows = slice((r * GL + w - GT) * P, (r * GL + w - GT + 1) * P)
+                    codes, scales = o_codes[:, rows].bitcast(E4M3), o_scales[:, rows]
                 nc.tensor.matmul_mx(
-                    out=acc[i, mt, h][:],
-                    lhsT=x_codes[i][:, w, rows].bitcast(E5M2 if w < GT else E4M3),
-                    lhsT_scale=x_scales[i][:, w, rows],
+                    out=banks[r, h][:],
+                    lhsT=codes,
+                    lhsT_scale=scales,
                     rhs=w_codes[w][:, cols].bitcast(E4M3),
                     rhs_scale=w_scales[w][:, cols],
                     start=(w == 0),
                     stop=(w == NW - 1),
                 )
 
-        def mx_all(i, passes):
-            for mt in range(2):
-                for h in range(2):
-                    mx(i, mt, h, passes)
-
         root = {}
         vel = {}
         vel2 = {}
         pw = {}
 
-        def root_d2(i, mt, h):
-            if (i, mt) not in root:
-                root[i, mt] = work.tile([P, N], F32, name="root", bufs=3)
-            nc.scalar.activation(out=root[i, mt][:, h * H:(h + 1) * H], in_=acc[i, mt, h][:], func=ACT.Sqrt)
+        def root_d2(r, h):
+            if r not in root:
+                root[r] = work.tile([P, N], F32, name="root", bufs=5)
+            nc.scalar.activation(out=root[r][:, h * H:(h + 1) * H], in_=banks[r, h][:], func=ACT.Sqrt)
+            give_bank((r, h))
 
-        def square_v(i, mt, c0=0, c1=N):
-            r = 2 * i + mt
-            if (i, mt) not in vel2:
-                vel2[i, mt] = work.tile([P, N], F32, name="vel2", bufs=2)
+        def square_v(r, c0=0, c1=N):
+            if r not in vel2:
+                vel2[r] = work.tile([P, N], F32, name="vel2", bufs=3)
             nc.scalar.activation(
-                out=vel2[i, mt][:, c0:c1], in_=root[i, mt][:, c0:c1], func=ACT.Square, scale=-1.0, bias=inflow_f[:, r:r + 1]
+                out=vel2[r][:, c0:c1], in_=root[r][:, c0:c1], func=ACT.Square, scale=-1.0, bias=inflow_f[:, r:r + 1]
             )
 
-        def speed_v(i, mt, c0=0, c1=N):
-            r = 2 * i + mt
-            if (i, mt) not in vel:
-                vel[i, mt] = work.tile([P, N], F32, name="vel", bufs=4)
+        def square_v_dve(r, c0, c1):
+            if r not in vel2:
+                vel2[r] = work.tile([P, N], F32, name="vel2", bufs=3)
+            nc.vector.tensor_tensor(out=vel2[r][:, c0:c1], in0=vel[r][:, c0:c1], in1=vel[r][:, c0:c1], op=ALU.mult)
+
+        def speed_v(r, c0=0, c1=N):
+            if r not in vel:
+                vel[r] = work.tile([P, N], F32, name="vel", bufs=3)
             nc.vector.tensor_scalar(
-                out=vel[i, mt][:, c0:c1], in0=root[i, mt][:, c0:c1], scalar1=-1.0, scalar2=inflow_f[:, r:r + 1],
+                out=vel[r][:, c0:c1], in0=root[r][:, c0:c1], scalar1=-1.0, scalar2=inflow_f[:, r:r + 1],
                 op0=ALU.mult, op1=ALU.add,
             )
-            nc.sync.dma_start(out=speed.rearrange("(p t) n -> p t n", t=ROWS)[:, r, c0:c1], in_=vel[i, mt][:, c0:c1])
+            nc.sync.dma_start(out=speed_rows[:, r, c0:c1], in_=vel[r][:, c0:c1])
 
-        def square_dve(i, mt, c0, c1):
-            nc.vector.tensor_tensor(
-                out=vel2[i, mt][:, c0:c1], in0=vel[i, mt][:, c0:c1], in1=vel[i, mt][:, c0:c1], op=ALU.mult
-            )
-
-        def power_v(i, mt, c0=0, c1=N):
-            r = 2 * i + mt
-            if (i, mt) not in pw:
-                pw[i, mt] = work.tile([P, N], F32, name="pw", bufs=4)
-            nc.vector.tensor_tensor(
-                out=pw[i, mt][:, c0:c1], in0=vel2[i, mt][:, c0:c1], in1=vel[i, mt][:, c0:c1], op=ALU.mult
-            )
-            nc.sync.dma_start(out=power.rearrange("(p t) n -> p t n", t=ROWS)[:, r, c0:c1], in_=pw[i, mt][:, c0:c1])
+        def power_v(r, c0=0, c1=N):
+            if r not in pw:
+                pw[r] = work.tile([P, N], F32, name="pw", bufs=3)
+            nc.vector.tensor_tensor(out=pw[r][:, c0:c1], in0=vel2[r][:, c0:c1], in1=vel[r][:, c0:c1], op=ALU.mult)
+            nc.sync.dma_start(out=power_rows[:, r, c0:c1], in_=pw[r][:, c0:c1])
 
         act_copy = nc.scalar.copy
         dve_copy = nc.vector.tensor_copy
 
-        load_w(0, 0, H)
-        load_t(0)
-        load_w(0, H, H)
-        load_o(0)
+        load_t(0, 1)
+        load_w(0, 0, Q)
+        load_t(1, 2)
+        load_t(2, 3)
+        load_w(0, Q, N)
         load_w(1, 0, N)
-        load_t(1)
+        load_o(0, 2)
         load_w(2, 0, N)
         load_w(3, 0, N)
-        load_o(1)
         load_w(4, 0, N)
-        load_t(2)
-        load_o(2)
+        load_o(2, 4)
+        load_t(3, 4)
+        nc.sync.dma_start(out=inflow_f[:], in_=inflow.rearrange("(p t) -> p t", t=ROWS))
+        load_t(4, 6)
+        load_o(4, 6)
+        load_t(6, 8)
+        load_o(6, 8)
 
-        lay(0, 0, act_copy, 0, Q)
-        lay(0, 0, dve_copy, Q, H)
-        turn_t(0, 0)
-        turn_t(0, 1)
-        square_t(0, 0)
-        square_t(0, 1)
-        quant_w(0, 0)
-        lay(0, 1, dve_copy)
-        turn_o(0, 0)
-        turn_o(0, 1)
-        turn_o(0, 2)
-        lay_o(0, 0, act_copy)
-        lay_o(0, 1, act_copy)
-        area_t(0, 0)
-        area_t(0, 1)
-        lay_o(0, 2, act_copy)
-        quant_w(0, 1)
-        lay(1, 1, act_copy)
-        lay(1, 0, dve_copy)
-        turn_t(1, 0)
-        turn_t(1, 1)
-        square_t(1, 0)
-        quant_t(0)
-        quant_o(0, 0)
-        quant_o(0, 1)
-        quant_w2(1)
-        for w in range(2):
-            mx_all(0, [w])
+        def mx_rows(rows, h, passes):
+            for w in passes:
+                for r in rows:
+                    mx(r, h, [w])
 
-        lay(2, 0, dve_copy)
-        lay(2, 1, act_copy)
-        square_t(1, 1)
-        turn_o(1, 0)
-        turn_o(1, 1)
-        turn_o(1, 2)
-        load_t(3)
-        load_o(3)
-        turn_t(2, 0)
-        lay(3, 0, dve_copy)
-        quant_w2(2)
-        lay(3, 1, act_copy)
-        lay_o(1, 0, act_copy)
-        lay_o(1, 1, act_copy)
-        lay_o(1, 2, dve_copy)
-        area_t(1, 0)
-        lay(4, 0, dve_copy)
-        quant_w2(3)
-        turn_t(2, 1)
-        turn_o(2, 0)
-        turn_o(2, 1)
-        for w in range(2, 4):
-            mx_all(0, [w])
-
-        lay(4, 1, act_copy)
-        square_t(2, 0)
-        square_t(2, 1)
-        turn_t(3, 0)
-        turn_t(3, 1)
-        turn_o(2, 2)
-        area_t(1, 1)
-        nc.vector.tensor_copy(out=inflow_f[:], in_=inflow_b[:])
-        quant_o(1, 0)
-        quant_o(1, 1)
-        quant_w2(4)
-        lay_o(2, 0, act_copy)
-        lay_o(2, 1, act_copy)
-        square_t(3, 0)
-        quant_t(1)
-        mx_all(0, [4])
-        area_t(2, 0)
-
-        groups = [(i, mt, h) for i in range(PAIRS) for mt in range(2) for h in range(2)]
-        for r in range(ROWS):
-            i, mt = divmod(r, 2)
-            last = r == ROWS - 1
+        def mx_tile(r, passes):
             for h in range(2):
-                root_d2(i, mt, h)
-                k = 2 * r + h + 4
-                if k < 2 * ROWS:
-                    mx(*groups[k], range(NW))
-                if last:
-                    speed_v(i, mt, h * H, (h + 1) * H)
-                    square_v(i, mt, h * H, (h + 1) * H)
-                    power_v(i, mt, h * H, (h + 1) * H)
-            if r == 0:
-                lay_o(2, 2, act_copy)
-            if r == 1:
-                square_t(3, 1)
-                lay_o(3, 0, act_copy)
-            if not last:
-                speed_v(i, mt)
-                square_v(i, mt)
-            if r == 0:
-                area_t(2, 1)
-                turn_o(3, 0)
-                turn_o(3, 1)
-                turn_o(3, 2)
-                quant_t(2)
-                quant_o(2, 0)
-                quant_o(2, 1)
-            if r == 1:
-                lay_o(3, 1, act_copy)
-                area_t(3, 0)
-                area_t(3, 1)
-            if r == 2:
-                lay_o(3, 2, act_copy)
-                quant_t(3)
-                quant_o(3, 0)
-                quant_o(3, 1)
-            if not last:
-                power_v(i, mt)
+                mx(r, h, passes)
+
+        turn_t(0)
+        turn_t(1)
+        turn_t(2)
+        square_t(0)
+        lay_w(0, 0, Q, dve_copy)
+        square_t(1)
+        area_t(0)
+        quant_w(0, 0, Q)
+        square_t(2)
+        area_t(1)
+        lay_w(0, Q, H, act_copy)
+        lay_w(0, H, N, act_copy)
+        area_t(2)
+        quant_t(0, 2)
+        quant_w(0, Q, H)
+        lay_w(1, 0, H, dve_copy)
+        quant_t(2, 3)
+        lay_w(1, H, N, act_copy)
+        turn_o(0)
+        turn_o(1)
+        turn_o(2)
+        quant_w(1, 0, H)
+        quant_w(0, H, N)
+        mx_rows([0, 1, 2], 0, [0, 1])
+        lay_o(0, act_copy)
+        lay_o(1, act_copy)
+        lay_o(2, act_copy)
+        lay_w(2, 0, H, dve_copy)
+        quant_w(1, H, N)
+        mx_rows([0, 1, 2], 1, [0, 1])
+        lay_w(2, H, N, act_copy)
+        quant_w(2, 0, H)
+        quant_o(0, 2)
+        lay_w(3, 0, H, dve_copy)
+        quant_o(2, 3)
+        mx_rows([0, 1], 0, [2])
+        quant_w(3, 0, H)
+        lay_w(3, H, N, act_copy)
+        quant_w(2, H, N)
+        mx_rows([0, 1], 0, [3])
+        mx_rows([0, 1], 1, [2])
+        lay_w(4, 0, H, dve_copy)
+        lay_w(4, H, W4_SPLIT, dve_copy)
+        turn_o(3)
+        turn_o(4)
+        quant_w(4, 0, H)
+        lay_w(4, W4_SPLIT, N, act_copy)
+        quant_w(3, H, N)
+        mx_rows([0, 1], 0, [4])
+        lay_o(3, act_copy)
+        lay_o(4, act_copy)
+        mx_rows([0, 1], 1, [3])
+        turn_t(3)
+        quant_w(4, H, N)
+        mx_rows([0, 1], 1, [4])
+        turn_o(5)
+        quant_o(3, 5)
+        root_d2(0, 0)
+        root_d2(0, 1)
+        mx_tile(2, [2, 3, 4])
+
+        def new_banks(q):
+            return [3 * q // 2 + 1] if q % 2 else [3 * q // 2, 3 * q // 2 + 1]
+
+        for s in range(ROWS):
+            q = s + 3
+            if q < ROWS:
+                square_t(q)
+            speed_v(s)
+            if q < ROWS:
+                first, last = new_banks(q)[0], new_banks(q)[-1]
+                if first != last:
+                    lay_o(first, dve_copy)
+                lay_o(last, act_copy)
+                area_t(q)
+                if q + 1 < ROWS:
+                    turn_t(q + 1)
+                    for b in new_banks(q + 1):
+                        turn_o(b)
+                quant_o(first, last + 1)
+                quant_t(q, q + 1)
+                mx(q, 0, range(NW))
+            if s < ROWS - 1:
+                square_v(s)
+                root_d2(s + 1, 0)
+                if q < ROWS:
+                    mx(q, 1, range(NW))
+                power_v(s)
+                root_d2(s + 1, 1)
+        square_v(7, 0, H)
+        power_v(7, 0, H)
+        square_v(7, H, N)
+        power_v(7, H, N)

@@ -24,7 +24,7 @@ ROWS = M // P
 PAIRS = ROWS // 2
 H = 512
 Q = 256
-W4_SPLIT = 736
+W4_SPLIT = 640
 
 
 def tile_wind_farm_wakes_s2_kernel(tc, thrust, area, kern, outer, okern, inflow, speed, power):
@@ -234,8 +234,8 @@ def tile_wind_farm_wakes_s2_kernel(tc, thrust, area, kern, outer, okern, inflow,
         load_o(0, 2)
         load_w(2, 0, N)
         load_w(3, 0, N)
-        load_w(4, 0, N)
         load_o(2, 4)
+        load_w(4, 0, N)
         load_t(3, 4)
         nc.sync.dma_start(out=inflow_f[:], in_=inflow.rearrange("(p t) -> p t", t=ROWS))
         load_t(4, 6)
@@ -270,78 +270,102 @@ def tile_wind_farm_wakes_s2_kernel(tc, thrust, area, kern, outer, okern, inflow,
         lay_w(1, 0, H, dve_copy)
         quant_t(2, 3)
         lay_w(1, H, N, act_copy)
+        mx_rows([0, 1], 0, [0])
         turn_o(0)
         turn_o(1)
         turn_o(2)
         quant_w(1, 0, H)
         quant_w(0, H, N)
-        mx_rows([0, 1, 2], 0, [0, 1])
+        mx_rows([2], 0, [0])
+        mx_rows([0, 1, 2], 0, [1])
+        mx_rows([0, 1], 1, [0])
         lay_o(0, act_copy)
+        mx_rows([2], 1, [0])
         lay_o(1, act_copy)
         lay_o(2, act_copy)
         lay_w(2, 0, H, dve_copy)
         quant_w(1, H, N)
-        mx_rows([0, 1, 2], 1, [0, 1])
+        mx_rows([0, 1, 2], 1, [1])
         lay_w(2, H, N, act_copy)
         quant_w(2, 0, H)
         quant_o(0, 2)
         lay_w(3, 0, H, dve_copy)
         quant_o(2, 3)
         mx_rows([0, 1], 0, [2])
+        turn_o(3)
+        turn_o(4)
         quant_w(3, 0, H)
         lay_w(3, H, N, act_copy)
         quant_w(2, H, N)
         mx_rows([0, 1], 0, [3])
         mx_rows([0, 1], 1, [2])
-        lay_w(4, 0, H, dve_copy)
-        lay_w(4, H, W4_SPLIT, dve_copy)
-        turn_o(3)
-        turn_o(4)
-        quant_w(4, 0, H)
-        lay_w(4, W4_SPLIT, N, act_copy)
-        quant_w(3, H, N)
-        mx_rows([0, 1], 0, [4])
-        lay_o(3, act_copy)
+        lay_o(3, dve_copy)
         lay_o(4, act_copy)
-        mx_rows([0, 1], 1, [3])
+        lay_w(4, 0, H, dve_copy)
         turn_t(3)
+        turn_o(5)
+        quant_w(3, H, N)
+        mx_rows([0, 1], 1, [3])
+        quant_o(3, 5)
+        mx_tile(2, [2, 3])
+        lay_w(4, H, W4_SPLIT, dve_copy)
+        lay_w(4, W4_SPLIT, N, act_copy)
+        quant_w(4, 0, H)
+        square_t(3)
+        lay_o(5, act_copy)
+        mx_rows([0, 1], 0, [4])
         quant_w(4, H, N)
         mx_rows([0, 1], 1, [4])
-        turn_o(5)
-        quant_o(3, 5)
+        mx_tile(2, [4])
+        turn_o(6)
+        turn_o(7)
+        area_t(3)
+        quant_o(5, 6)
         root_d2(0, 0)
+        turn_t(4)
+        quant_t(3, 4)
         root_d2(0, 1)
-        mx_tile(2, [2, 3, 4])
+        root_d2(1, 0)
+        speed_v(0)
+        lay_o(6, dve_copy)
+        square_v(0)
+        lay_o(7, dve_copy)
 
         def new_banks(q):
             return [3 * q // 2 + 1] if q % 2 else [3 * q // 2, 3 * q // 2 + 1]
 
-        for s in range(ROWS):
+        for s in range(1, ROWS - 1):
             q = s + 3
             if q < ROWS:
                 square_t(q)
+            if q == 4:
+                quant_o(6, 8)
+            elif q < ROWS and q % 2 == 0:
+                lay_o(new_banks(q)[0], dve_copy)
+            root_d2(s, 1)
+            power_v(s - 1)
+            if q + 1 < ROWS:
+                turn_t(q + 1)
+                for b in new_banks(q + 1):
+                    turn_o(b)
+            if s + 2 < ROWS:
+                mx_tile(s + 2, range(NW))
+            root_d2(s + 1, 0)
+            if 4 < q < ROWS:
+                lay_o(new_banks(q)[-1], act_copy)
+            if q < ROWS:
+                area_t(q)
             speed_v(s)
             if q < ROWS:
-                first, last = new_banks(q)[0], new_banks(q)[-1]
-                if first != last:
-                    lay_o(first, dve_copy)
-                lay_o(last, act_copy)
-                area_t(q)
-                if q + 1 < ROWS:
-                    turn_t(q + 1)
-                    for b in new_banks(q + 1):
-                        turn_o(b)
-                quant_o(first, last + 1)
                 quant_t(q, q + 1)
-                mx(q, 0, range(NW))
-            if s < ROWS - 1:
-                square_v(s)
-                root_d2(s + 1, 0)
-                if q < ROWS:
-                    mx(q, 1, range(NW))
-                power_v(s)
-                root_d2(s + 1, 1)
+            if 4 < q < ROWS:
+                quant_o(new_banks(q)[0], new_banks(q)[-1] + 1)
+            square_v(s)
         square_v(7, 0, H)
+        root_d2(7, 1)
+        power_v(6)
+        speed_v(7, 0, H)
         power_v(7, 0, H)
+        speed_v(7, H, N)
         square_v(7, H, N)
         power_v(7, H, N)

@@ -24,7 +24,13 @@ ROWS = M // P
 PAIRS = ROWS // 2
 H = 512
 Q = 256
-W4_SPLIT = 640
+LATE = 5
+W4_SPLIT = 704
+EXT_FIRST = 4
+AREA_AT = {2: 5, 4: 6, 5: 7}
+MX_AT = {2: 5, 4: 6, 5: 7}
+OWN = [0, 1]
+EXT = [2, 3, 4]
 
 
 def tile_wind_farm_wakes_s2_kernel(tc, thrust, area, kern, outer, okern, inflow, speed, power):
@@ -126,7 +132,7 @@ def tile_wind_farm_wakes_s2_kernel(tc, thrust, area, kern, outer, okern, inflow,
         o_lay = {}
 
         def square_t(r):
-            t_sq[r] = work.tile([P, 2 * P, 4], F32, name="t_sq", bufs=3, align_bytes=64)
+            t_sq[r] = work.tile([P, 2 * P, 4], F32, name="t_sq", bufs=4, align_bytes=64)
             nc.scalar.activation(
                 out=t_sq[r][:].rearrange("p c (u e) -> p c u e", e=2),
                 in_=banks["t", r][:].bitcast(BF16).rearrange("p u (c e) -> p c u e", e=2),
@@ -167,6 +173,7 @@ def tile_wind_farm_wakes_s2_kernel(tc, thrust, area, kern, outer, okern, inflow,
             if (r, h) not in banks:
                 take_bank((r, h), [P, H])
             cols = slice(h * H, (h + 1) * H)
+            order = OWN + EXT if r < EXT_FIRST else EXT + OWN
             for w in passes:
                 if w < GT:
                     rows = slice((r * GT + w) * P, (r * GT + w + 1) * P)
@@ -180,8 +187,8 @@ def tile_wind_farm_wakes_s2_kernel(tc, thrust, area, kern, outer, okern, inflow,
                     lhsT_scale=scales,
                     rhs=w_codes[w][:, cols].bitcast(E4M3),
                     rhs_scale=w_scales[w][:, cols],
-                    start=(w == 0),
-                    stop=(w == NW - 1),
+                    start=(w == order[0]),
+                    stop=(w == order[-1]),
                 )
 
         root = {}
@@ -191,7 +198,7 @@ def tile_wind_farm_wakes_s2_kernel(tc, thrust, area, kern, outer, okern, inflow,
 
         def root_d2(r, h):
             if r not in root:
-                root[r] = work.tile([P, N], F32, name="root", bufs=5)
+                root[r] = work.tile([P, N], F32, name="root", bufs=4)
             nc.scalar.activation(out=root[r][:, h * H:(h + 1) * H], in_=banks[r, h][:], func=ACT.Sqrt)
             give_bank((r, h))
 
@@ -226,20 +233,20 @@ def tile_wind_farm_wakes_s2_kernel(tc, thrust, area, kern, outer, okern, inflow,
         dve_copy = nc.vector.tensor_copy
 
         load_t(0, 1)
-        load_w(0, 0, Q)
         load_t(1, 2)
+        load_w(0, 0, Q)
         load_t(2, 3)
+        load_t(3, 4)
         load_w(0, Q, N)
-        load_w(1, 0, N)
+        load_t(4, 6)
         load_o(0, 2)
+        load_w(1, 0, N)
+        load_o(2, 4)
         load_w(2, 0, N)
         load_w(3, 0, N)
-        load_o(2, 4)
         load_w(4, 0, N)
-        load_t(3, 4)
-        nc.sync.dma_start(out=inflow_f[:], in_=inflow.rearrange("(p t) -> p t", t=ROWS))
-        load_t(4, 6)
         load_o(4, 6)
+        nc.sync.dma_start(out=inflow_f[:], in_=inflow.rearrange("(p t) -> p t", t=ROWS))
         load_t(6, 8)
         load_o(6, 8)
 
@@ -252,120 +259,129 @@ def tile_wind_farm_wakes_s2_kernel(tc, thrust, area, kern, outer, okern, inflow,
             for h in range(2):
                 mx(r, h, passes)
 
-        turn_t(0)
-        turn_t(1)
-        turn_t(2)
+        for r in range(4):
+            turn_t(r)
         square_t(0)
         lay_w(0, 0, Q, dve_copy)
+        quant_w(0, 0, Q)
         square_t(1)
         area_t(0)
-        quant_w(0, 0, Q)
         square_t(2)
         area_t(1)
-        lay_w(0, Q, H, act_copy)
-        lay_w(0, H, N, act_copy)
-        area_t(2)
+        square_t(3)
+        lay_w(0, Q, H, dve_copy)
         quant_t(0, 2)
+        lay_w(0, H, H + Q, dve_copy)
+        lay_w(0, H + Q, N, act_copy)
+        turn_t(4)
+        turn_t(5)
+        area_t(2)
+        square_t(4)
         quant_w(0, Q, H)
-        lay_w(1, 0, H, dve_copy)
-        quant_t(2, 3)
-        lay_w(1, H, N, act_copy)
-        mx_rows([0, 1], 0, [0])
-        turn_o(0)
-        turn_o(1)
-        turn_o(2)
-        quant_w(1, 0, H)
+        area_t(3)
         quant_w(0, H, N)
-        mx_rows([2], 0, [0])
-        mx_rows([0, 1, 2], 0, [1])
+        square_t(5)
+        for b in range(3):
+            turn_o(b)
+        mx_rows([0, 1], 0, [0])
         mx_rows([0, 1], 1, [0])
-        lay_o(0, act_copy)
-        mx_rows([2], 1, [0])
-        lay_o(1, act_copy)
-        lay_o(2, act_copy)
-        lay_w(2, 0, H, dve_copy)
-        quant_w(1, H, N)
-        mx_rows([0, 1, 2], 1, [1])
-        lay_w(2, H, N, act_copy)
-        quant_w(2, 0, H)
+        quant_t(2, 4)
+        for b in range(3):
+            lay_o(b, act_copy)
+        lay_w(1, 0, H, dve_copy)
+        lay_w(1, H, N, act_copy)
         quant_o(0, 2)
-        lay_w(3, 0, H, dve_copy)
+        quant_w(1, 0, H)
+        for b in range(3, 6):
+            turn_o(b)
+        mx_rows([0, 1], 0, [1])
         quant_o(2, 3)
-        mx_rows([0, 1], 0, [2])
-        turn_o(3)
-        turn_o(4)
-        quant_w(3, 0, H)
-        lay_w(3, H, N, act_copy)
-        quant_w(2, H, N)
-        mx_rows([0, 1], 0, [3])
-        mx_rows([0, 1], 1, [2])
-        lay_o(3, dve_copy)
-        lay_o(4, act_copy)
-        lay_w(4, 0, H, dve_copy)
-        turn_t(3)
-        turn_o(5)
-        quant_w(3, H, N)
-        mx_rows([0, 1], 1, [3])
+        quant_w(1, H, N)
+        mx_rows([0, 1], 1, [1])
+        for b in range(3, 6):
+            lay_o(b, act_copy)
+        mx_tile(2, OWN)
+        lay_w(2, 0, H, dve_copy)
+        lay_w(2, H, N, act_copy)
         quant_o(3, 5)
-        mx_tile(2, [2, 3])
+        quant_w(2, 0, H)
+        mx_rows([0, 1, 2], 0, [2])
+        lay_w(3, 0, H, dve_copy)
+        lay_w(3, H, N, act_copy)
+        quant_o(5, 6)
+        quant_w(3, 0, H)
+        mx_rows([0, 1, 2], 0, [3])
+        quant_w(2, H, N)
+        mx_rows([0, 1, 2], 1, [2])
+        lay_w(4, 0, H, dve_copy)
         lay_w(4, H, W4_SPLIT, dve_copy)
         lay_w(4, W4_SPLIT, N, act_copy)
+        turn_o(6)
+        turn_o(7)
+        quant_w(3, H, N)
+        mx_rows([0, 1, 2], 1, [3])
         quant_w(4, 0, H)
-        square_t(3)
-        lay_o(5, act_copy)
+        lay_o(6, act_copy)
+        lay_o(7, act_copy)
         mx_rows([0, 1], 0, [4])
         quant_w(4, H, N)
         mx_rows([0, 1], 1, [4])
         mx_tile(2, [4])
-        turn_o(6)
-        turn_o(7)
-        area_t(3)
-        quant_o(5, 6)
+        turn_o(8)
+        area_t(4)
         root_d2(0, 0)
-        turn_t(4)
-        quant_t(3, 4)
-        root_d2(0, 1)
-        root_d2(1, 0)
-        speed_v(0)
-        lay_o(6, dve_copy)
-        square_v(0)
-        lay_o(7, dve_copy)
+        mx_tile(3, range(NW))
+        quant_o(6, 8)
+        quant_t(4, 5)
 
-        def new_banks(q):
-            return [3 * q // 2 + 1] if q % 2 else [3 * q // 2, 3 * q // 2 + 1]
-
-        for s in range(1, ROWS - 1):
-            q = s + 3
-            if q < ROWS:
-                square_t(q)
-            if q == 4:
-                quant_o(6, 8)
-            elif q < ROWS and q % 2 == 0:
-                lay_o(new_banks(q)[0], dve_copy)
+        for s in range(ROWS - 1):
             root_d2(s, 1)
-            power_v(s - 1)
-            if q + 1 < ROWS:
-                turn_t(q + 1)
-                for b in new_banks(q + 1):
-                    turn_o(b)
-            if s + 2 < ROWS:
-                mx_tile(s + 2, range(NW))
-            root_d2(s + 1, 0)
-            if 4 < q < ROWS:
-                lay_o(new_banks(q)[-1], act_copy)
-            if q < ROWS:
-                area_t(q)
+            if s == 0:
+                mx(4, 0, EXT + OWN)
+            if s < LATE:
+                root_d2(s + 1, 0)
+            if s == 1:
+                turn_o(9)
+                turn_o(10)
+                turn_t(6)
+                mx(4, 1, EXT + OWN)
+            if s == 3:
+                turn_o(11)
+                turn_t(7)
+            if s in AREA_AT:
+                area_t(AREA_AT[s])
+            if s in MX_AT:
+                mx_tile(MX_AT[s], EXT)
             speed_v(s)
-            if q < ROWS:
-                quant_t(q, q + 1)
-            if 4 < q < ROWS:
-                quant_o(new_banks(q)[0], new_banks(q)[-1] + 1)
+            if s == 0:
+                lay_o(8, dve_copy)
+            if s in AREA_AT:
+                quant_t(AREA_AT[s], AREA_AT[s] + 1)
+            if s in MX_AT:
+                mx_tile(MX_AT[s], OWN)
             square_v(s)
-        square_v(7, 0, H)
+            if s >= LATE:
+                root_d2(s + 1, 0)
+            if s == 3:
+                lay_o(9, dve_copy)
+                lay_o(10, act_copy)
+                square_t(6)
+            if s == 4:
+                lay_o(11, act_copy)
+                square_t(7)
+            power_v(s)
+            if s == 0:
+                quant_o(8, 9)
+            if s == 3:
+                quant_o(9, 11)
+            if s == 4:
+                quant_o(11, 12)
         root_d2(7, 1)
-        power_v(6)
         speed_v(7, 0, H)
-        power_v(7, 0, H)
+        square_v(7, 0, H)
         speed_v(7, H, N)
-        square_v(7, H, N)
-        power_v(7, H, N)
+        square_v(7, H, H + Q)
+        power_v(7, 0, H)
+        square_v(7, H + Q, N)
+        power_v(7, H, H + Q)
+        power_v(7, H + Q, N)

@@ -25,10 +25,12 @@ PAIRS = ROWS // 2
 H = 512
 Q = 256
 LATE = 5
-W4_SPLIT = 704
 EXT_FIRST = 4
 AREA_AT = {2: 5, 4: 6, 5: 7}
 MX_AT = {2: 5, 4: 6, 5: 7}
+S0 = 704
+WL = 5
+RB = 5
 OWN = [0, 1]
 EXT = [2, 3, 4]
 
@@ -43,7 +45,6 @@ def tile_wind_farm_wakes_s2_kernel(tc, thrust, area, kern, outer, okern, inflow,
 
         area_b = keep.tile([P, GT, 4], BF16, name="area_b")
         inflow_f = keep.tile([P, ROWS], BF16, name="inflow_f")
-        nc.scalar.dma_start(out=area_b[:], in_=area.rearrange("(g p j) -> p g j", g=GT, j=4))
         dummy = keep.tile([P, 1], F32, name="dummy")
         nc.gpsimd.memset(dummy[:], 1.0)
         nc.scalar.activation(out=dummy[:], in_=dummy[:], func=ACT.Sqrt)
@@ -60,19 +61,19 @@ def tile_wind_farm_wakes_s2_kernel(tc, thrust, area, kern, outer, okern, inflow,
         o_raw = {}
 
         def load_w(w, c0, c1):
-            raw = keep.tile([P, 4, c1 - c0], BF16, name="w_raw_%d_%d" % (w, c0), align_bytes=64)
+            raw = keep.tile([P, 4, c1 - c0], BF16, name="raw_w%d_%d" % (w, c0), align_bytes=64)
             nc.sync.dma_start(out=raw[:], in_=w_hbm[w].rearrange("(p j) n -> p j n", j=4)[:, :, c0:c1])
             for c in range(c0, c1, 32):
                 w_raw[w, c] = raw[:, :, c - c0:]
 
-        def load_t(r0, r1):
-            raw = keep.tile([P, r1 - r0, T], BF16, name="t_raw_%d" % r0, align_bytes=64)
+        def load_t(r0, r1, slot=None):
+            raw = keep.tile([P, r1 - r0, T], BF16, name=slot or "raw_t%d" % r0, align_bytes=64)
             nc.sync.dma_start(out=raw[:], in_=thrust_rows[:, r0:r1, :])
             for r in range(r0, r1):
                 t_raw[r] = raw[:, r - r0, :]
 
-        def load_o(r0, r1):
-            raw = keep.tile([P, r1 - r0, L], BF16, name="o_raw_%d" % r0, align_bytes=64)
+        def load_o(r0, r1, slot=None):
+            raw = keep.tile([P, r1 - r0, L], BF16, name=slot or "raw_o%d" % r0, align_bytes=64)
             nc.sync.dma_start(out=raw[:], in_=outer_rows[:, r0:r1, :])
             for r in range(r0, r1):
                 o_raw[r] = raw[:, r - r0, :]
@@ -84,7 +85,7 @@ def tile_wind_farm_wakes_s2_kernel(tc, thrust, area, kern, outer, okern, inflow,
         def lay_w(w, c0, c1, copy):
             h = c0 // H
             if (w, h) not in w_lay:
-                w_lay[w, h] = work.tile([P, H, 4], BF16, name="w_lay", bufs=4, align_bytes=64)
+                w_lay[w, h] = work.tile([P, H, 4], BF16, name="w_lay", bufs=WL, align_bytes=64)
             copy(
                 out=w_lay[w, h][:, c0 - h * H:c1 - h * H].rearrange("p (c i) j -> p c j i", i=4),
                 in_=w_raw[w, c0][:, :, 0:c1 - c0].rearrange("p j (c i) -> p c j i", i=4),
@@ -159,7 +160,7 @@ def tile_wind_farm_wakes_s2_kernel(tc, thrust, area, kern, outer, okern, inflow,
             )
 
         def lay_o(b, copy):
-            if b % GL == 0:
+            if b // GL not in o_lay:
                 o_lay[b // GL] = work.tile([P, GL, 2 * P, 2], F32, name="o_lay", bufs=2, align_bytes=64)
             copy(out=o_lay[b // GL][:, b % GL], in_=banks["o", b][:].rearrange("p u c -> p c u"))
             give_bank(("o", b))
@@ -198,7 +199,7 @@ def tile_wind_farm_wakes_s2_kernel(tc, thrust, area, kern, outer, okern, inflow,
 
         def root_d2(r, h):
             if r not in root:
-                root[r] = work.tile([P, N], F32, name="root", bufs=4)
+                root[r] = work.tile([P, N], F32, name="root", bufs=RB)
             nc.scalar.activation(out=root[r][:, h * H:(h + 1) * H], in_=banks[r, h][:], func=ACT.Sqrt)
             give_bank((r, h))
 
@@ -216,7 +217,7 @@ def tile_wind_farm_wakes_s2_kernel(tc, thrust, area, kern, outer, okern, inflow,
 
         def speed_v(r, c0=0, c1=N):
             if r not in vel:
-                vel[r] = work.tile([P, N], F32, name="vel", bufs=3)
+                vel[r] = work.tile([P, N], F32, name="vel", bufs=4)
             nc.vector.tensor_scalar(
                 out=vel[r][:, c0:c1], in0=root[r][:, c0:c1], scalar1=-1.0, scalar2=inflow_f[:, r:r + 1],
                 op0=ALU.mult, op1=ALU.add,
@@ -235,6 +236,7 @@ def tile_wind_farm_wakes_s2_kernel(tc, thrust, area, kern, outer, okern, inflow,
         load_t(0, 1)
         load_t(1, 2)
         load_w(0, 0, Q)
+        nc.sync.dma_start(out=area_b[:], in_=area.rearrange("(g p j) -> p g j", g=GT, j=4))
         load_t(2, 3)
         load_t(3, 4)
         load_w(0, Q, N)
@@ -247,8 +249,6 @@ def tile_wind_farm_wakes_s2_kernel(tc, thrust, area, kern, outer, okern, inflow,
         load_w(4, 0, N)
         load_o(4, 6)
         nc.sync.dma_start(out=inflow_f[:], in_=inflow.rearrange("(p t) -> p t", t=ROWS))
-        load_t(6, 8)
-        load_o(6, 8)
 
         def mx_rows(rows, h, passes):
             for w in passes:
@@ -271,8 +271,9 @@ def tile_wind_farm_wakes_s2_kernel(tc, thrust, area, kern, outer, okern, inflow,
         square_t(3)
         lay_w(0, Q, H, dve_copy)
         quant_t(0, 2)
-        lay_w(0, H, H + Q, dve_copy)
-        lay_w(0, H + Q, N, act_copy)
+        lay_w(0, H, S0, dve_copy)
+        lay_w(0, S0, N, act_copy)
+        load_t(6, 8, "raw_w0_256")
         turn_t(4)
         turn_t(5)
         area_t(2)
@@ -290,6 +291,7 @@ def tile_wind_farm_wakes_s2_kernel(tc, thrust, area, kern, outer, okern, inflow,
             lay_o(b, act_copy)
         lay_w(1, 0, H, dve_copy)
         lay_w(1, H, N, act_copy)
+        load_o(6, 8, "raw_w1_0")
         quant_o(0, 2)
         quant_w(1, 0, H)
         for b in range(3, 6):
@@ -308,80 +310,95 @@ def tile_wind_farm_wakes_s2_kernel(tc, thrust, area, kern, outer, okern, inflow,
         mx_rows([0, 1, 2], 0, [2])
         lay_w(3, 0, H, dve_copy)
         lay_w(3, H, N, act_copy)
-        quant_o(5, 6)
-        quant_w(3, 0, H)
-        mx_rows([0, 1, 2], 0, [3])
         quant_w(2, H, N)
+        quant_w(3, 0, H)
         mx_rows([0, 1, 2], 1, [2])
+        mx_rows([0, 1, 2], 0, [3])
         lay_w(4, 0, H, dve_copy)
-        lay_w(4, H, W4_SPLIT, dve_copy)
-        lay_w(4, W4_SPLIT, N, act_copy)
+        lay_w(4, H, N, act_copy)
         turn_o(6)
         turn_o(7)
         quant_w(3, H, N)
-        mx_rows([0, 1, 2], 1, [3])
         quant_w(4, 0, H)
+        mx_rows([0, 1], 1, [3])
+        mx_rows([0, 1, 2], 0, [4])
+        quant_o(5, 6)
         lay_o(6, act_copy)
         lay_o(7, act_copy)
-        mx_rows([0, 1], 0, [4])
         quant_w(4, H, N)
         mx_rows([0, 1], 1, [4])
-        mx_tile(2, [4])
-        turn_o(8)
+        mx(2, 1, [3, 4])
         area_t(4)
         root_d2(0, 0)
+        root_d2(1, 0)
+        turn_o(8)
+        root_d2(0, 1)
         mx_tile(3, range(NW))
         quant_o(6, 8)
         quant_t(4, 5)
-
-        for s in range(ROWS - 1):
-            root_d2(s, 1)
-            if s == 0:
-                mx(4, 0, EXT + OWN)
-            if s < LATE:
-                root_d2(s + 1, 0)
-            if s == 1:
-                turn_o(9)
-                turn_o(10)
-                turn_t(6)
-                mx(4, 1, EXT + OWN)
-            if s == 3:
-                turn_o(11)
-                turn_t(7)
-            if s in AREA_AT:
-                area_t(AREA_AT[s])
-            if s in MX_AT:
-                mx_tile(MX_AT[s], EXT)
-            speed_v(s)
-            if s == 0:
-                lay_o(8, dve_copy)
-            if s in AREA_AT:
-                quant_t(AREA_AT[s], AREA_AT[s] + 1)
-            if s in MX_AT:
-                mx_tile(MX_AT[s], OWN)
-            square_v(s)
-            if s >= LATE:
-                root_d2(s + 1, 0)
-            if s == 3:
-                lay_o(9, dve_copy)
-                lay_o(10, act_copy)
-                square_t(6)
-            if s == 4:
-                lay_o(11, act_copy)
-                square_t(7)
-            power_v(s)
-            if s == 0:
-                quant_o(8, 9)
-            if s == 3:
-                quant_o(9, 11)
-            if s == 4:
-                quant_o(11, 12)
+        root_d2(1, 1)
+        speed_v(0)
+        square_v(0)
+        speed_v(1)
+        area_t(5)
+        square_v(1)
+        mx(4, 0, EXT + OWN)
+        root_d2(2, 0)
+        root_d2(2, 1)
+        power_v(0)
+        quant_t(5, 6)
+        lay_o(8, act_copy)
+        turn_o(9)
+        turn_o(10)
+        turn_t(6)
+        mx(4, 1, EXT + OWN)
+        power_v(1)
+        speed_v(2)
+        quant_o(8, 9)
+        square_v(2)
+        power_v(2)
+        root_d2(3, 0)
+        root_d2(3, 1)
+        turn_o(11)
+        turn_t(7)
+        speed_v(3)
+        lay_o(10, act_copy)
+        lay_o(9, dve_copy)
+        mx_tile(5, EXT + OWN)
+        square_v(3)
+        square_t(6)
+        power_v(3)
+        quant_o(9, 11)
+        mx_tile(6, EXT)
+        area_t(6)
+        root_d2(4, 0)
+        root_d2(4, 1)
+        speed_v(4)
+        quant_t(6, 7)
+        mx_tile(6, OWN)
+        lay_o(11, act_copy)
+        square_v(4)
+        square_t(7)
+        power_v(4)
+        quant_o(11, 12)
+        mx_tile(7, EXT)
+        area_t(7)
+        root_d2(5, 0)
+        root_d2(5, 1)
+        speed_v(5)
+        quant_t(7, 8)
+        mx_tile(7, OWN)
+        root_d2(6, 0)
+        root_d2(6, 1)
+        square_v(5)
+        speed_v(6)
+        power_v(5)
+        square_v(6)
+        power_v(6)
+        root_d2(7, 0)
         root_d2(7, 1)
-        speed_v(7, 0, H)
+        speed_v(7)
         square_v(7, 0, H)
-        speed_v(7, H, N)
-        square_v(7, H, H + Q)
+        square_v(7, H, N)
         power_v(7, 0, H)
-        square_v(7, H + Q, N)
-        power_v(7, H, H + Q)
-        power_v(7, H + Q, N)
+        power_v(7, H, N)

@@ -29,8 +29,13 @@ EXT_FIRST = 4
 AREA_AT = {2: 5, 4: 6, 5: 7}
 MX_AT = {2: 5, 4: 6, 5: 7}
 S0 = 704
-WL = 5
+WL = 7
 RB = 5
+OUT_SLOTS = ["lay_w0", "lay_w1", "raw_w2_0", "raw_w3_0", "raw_w4_0", "lay_w2", "lay_w3", "lay_w4"]
+S1 = 576
+S2 = 512
+S3 = 512
+S4 = 640
 OWN = [0, 1]
 EXT = [2, 3, 4]
 
@@ -83,11 +88,10 @@ def tile_wind_farm_wakes_s2_kernel(tc, thrust, area, kern, outer, okern, inflow,
         w_lay = {}
 
         def lay_w(w, c0, c1, copy):
-            h = c0 // H
-            if (w, h) not in w_lay:
-                w_lay[w, h] = work.tile([P, H, 4], BF16, name="w_lay", bufs=WL, align_bytes=64)
+            if w not in w_lay:
+                w_lay[w] = keep.tile([P, N, 4], BF16, name="lay_w%d" % w, align_bytes=64)
             copy(
-                out=w_lay[w, h][:, c0 - h * H:c1 - h * H].rearrange("p (c i) j -> p c j i", i=4),
+                out=w_lay[w][:, c0:c1].rearrange("p (c i) j -> p c j i", i=4),
                 in_=w_raw[w, c0][:, :, 0:c1 - c0].rearrange("p j (c i) -> p c j i", i=4),
             )
 
@@ -95,7 +99,7 @@ def tile_wind_farm_wakes_s2_kernel(tc, thrust, area, kern, outer, okern, inflow,
             nc.vector.quantize_mx(
                 out=w_codes[w][:, c0:c1].bitcast(E4M3),
                 scales=w_scales[w][:, c0:c1],
-                in_=w_lay[w, c0 // H][:, c0 % H:c0 % H + c1 - c0].rearrange("p c j -> p (c j)"),
+                in_=w_lay[w][:, c0:c1].rearrange("p c j -> p (c j)"),
             )
 
         a_codes = keep.tile([P, ROWS * GT * P], U32, name="a_codes", align_bytes=64)
@@ -130,10 +134,10 @@ def tile_wind_farm_wakes_s2_kernel(tc, thrust, area, kern, outer, okern, inflow,
 
         t_sq = {}
         t_a = {}
-        o_lay = {}
+        o_lay = keep.tile([P, ROWS * GL // 2, 2 * P, 2], F32, name="o_lay", align_bytes=64)
 
         def square_t(r):
-            t_sq[r] = work.tile([P, 2 * P, 4], F32, name="t_sq", bufs=4, align_bytes=64)
+            t_sq[r] = work.tile([P, 2 * P, 4], F32, name="t_sq", bufs=6, align_bytes=64)
             nc.scalar.activation(
                 out=t_sq[r][:].rearrange("p c (u e) -> p c u e", e=2),
                 in_=banks["t", r][:].bitcast(BF16).rearrange("p u (c e) -> p c u e", e=2),
@@ -160,14 +164,12 @@ def tile_wind_farm_wakes_s2_kernel(tc, thrust, area, kern, outer, okern, inflow,
             )
 
         def lay_o(b, copy):
-            if b // GL not in o_lay:
-                o_lay[b // GL] = work.tile([P, GL, 2 * P, 2], F32, name="o_lay", bufs=2, align_bytes=64)
-            copy(out=o_lay[b // GL][:, b % GL], in_=banks["o", b][:].rearrange("p u c -> p c u"))
+            copy(out=o_lay[:, b], in_=banks["o", b][:].rearrange("p u c -> p c u"))
             give_bank(("o", b))
 
         def quant_o(b0, b1):
             cols = slice(b0 * 2 * P, b1 * 2 * P)
-            src = o_lay[b0 // GL][:, b0 % GL:b0 % GL + b1 - b0].rearrange("p g c u -> p (g c u)").bitcast(BF16)
+            src = o_lay[:, b0:b1].rearrange("p g c u -> p (g c u)").bitcast(BF16)
             nc.vector.quantize_mx(out=o_codes[:, cols].bitcast(E4M3), scales=o_scales[:, cols], in_=src)
 
         def mx(r, h, passes):
@@ -192,6 +194,15 @@ def tile_wind_farm_wakes_s2_kernel(tc, thrust, area, kern, outer, okern, inflow,
                     stop=(w == order[-1]),
                 )
 
+        spare = []
+
+        def out_tile(k):
+            if not spare:
+                both = keep.tile([P, 2, N], F32, name=OUT_SLOTS[(len(vel) + len(pw)) // 2], align_bytes=64)
+                spare.append(both[:, 1, :])
+                return both[:, 0, :]
+            return spare.pop()
+
         root = {}
         vel = {}
         vel2 = {}
@@ -205,19 +216,19 @@ def tile_wind_farm_wakes_s2_kernel(tc, thrust, area, kern, outer, okern, inflow,
 
         def square_v(r, c0=0, c1=N):
             if r not in vel2:
-                vel2[r] = work.tile([P, N], F32, name="vel2", bufs=3)
+                vel2[r] = work.tile([P, N], F32, name="t_sq", bufs=6, align_bytes=64)
             nc.scalar.activation(
                 out=vel2[r][:, c0:c1], in_=root[r][:, c0:c1], func=ACT.Square, scale=-1.0, bias=inflow_f[:, r:r + 1]
             )
 
         def square_v_dve(r, c0, c1):
             if r not in vel2:
-                vel2[r] = work.tile([P, N], F32, name="vel2", bufs=3)
+                vel2[r] = work.tile([P, N], F32, name="t_sq", bufs=6, align_bytes=64)
             nc.vector.tensor_tensor(out=vel2[r][:, c0:c1], in0=vel[r][:, c0:c1], in1=vel[r][:, c0:c1], op=ALU.mult)
 
         def speed_v(r, c0=0, c1=N):
             if r not in vel:
-                vel[r] = work.tile([P, N], F32, name="vel", bufs=4)
+                vel[r] = out_tile(2 * r)
             nc.vector.tensor_scalar(
                 out=vel[r][:, c0:c1], in0=root[r][:, c0:c1], scalar1=-1.0, scalar2=inflow_f[:, r:r + 1],
                 op0=ALU.mult, op1=ALU.add,
@@ -226,7 +237,7 @@ def tile_wind_farm_wakes_s2_kernel(tc, thrust, area, kern, outer, okern, inflow,
 
         def power_v(r, c0=0, c1=N):
             if r not in pw:
-                pw[r] = work.tile([P, N], F32, name="pw", bufs=3)
+                pw[r] = out_tile(2 * r + 1)
             nc.vector.tensor_tensor(out=pw[r][:, c0:c1], in0=vel2[r][:, c0:c1], in1=vel[r][:, c0:c1], op=ALU.mult)
             nc.sync.dma_start(out=power_rows[:, r, c0:c1], in_=pw[r][:, c0:c1])
 
@@ -239,6 +250,7 @@ def tile_wind_farm_wakes_s2_kernel(tc, thrust, area, kern, outer, okern, inflow,
         nc.sync.dma_start(out=area_b[:], in_=area.rearrange("(g p j) -> p g j", g=GT, j=4))
         load_t(2, 3)
         load_t(3, 4)
+        nc.sync.dma_start(out=inflow_f[:], in_=inflow.rearrange("(p t) -> p t", t=ROWS))
         load_w(0, Q, N)
         load_t(4, 6)
         load_o(0, 2)
@@ -248,7 +260,6 @@ def tile_wind_farm_wakes_s2_kernel(tc, thrust, area, kern, outer, okern, inflow,
         load_w(3, 0, N)
         load_w(4, 0, N)
         load_o(4, 6)
-        nc.sync.dma_start(out=inflow_f[:], in_=inflow.rearrange("(p t) -> p t", t=ROWS))
 
         def mx_rows(rows, h, passes):
             for w in passes:
@@ -269,9 +280,8 @@ def tile_wind_farm_wakes_s2_kernel(tc, thrust, area, kern, outer, okern, inflow,
         square_t(2)
         area_t(1)
         square_t(3)
-        lay_w(0, Q, H, dve_copy)
+        lay_w(0, Q, S0, dve_copy)
         quant_t(0, 2)
-        lay_w(0, H, S0, dve_copy)
         lay_w(0, S0, N, act_copy)
         load_t(6, 8, "raw_w0_256")
         turn_t(4)
@@ -289,8 +299,8 @@ def tile_wind_farm_wakes_s2_kernel(tc, thrust, area, kern, outer, okern, inflow,
         quant_t(2, 4)
         for b in range(3):
             lay_o(b, act_copy)
-        lay_w(1, 0, H, dve_copy)
-        lay_w(1, H, N, act_copy)
+        lay_w(1, 0, S1, dve_copy)
+        lay_w(1, S1, N, act_copy)
         load_o(6, 8, "raw_w1_0")
         quant_o(0, 2)
         quant_w(1, 0, H)
@@ -303,19 +313,19 @@ def tile_wind_farm_wakes_s2_kernel(tc, thrust, area, kern, outer, okern, inflow,
         for b in range(3, 6):
             lay_o(b, act_copy)
         mx_tile(2, OWN)
-        lay_w(2, 0, H, dve_copy)
-        lay_w(2, H, N, act_copy)
+        lay_w(2, 0, S2, dve_copy)
+        lay_w(2, S2, N, act_copy)
         quant_o(3, 5)
         quant_w(2, 0, H)
         mx_rows([0, 1, 2], 0, [2])
-        lay_w(3, 0, H, dve_copy)
-        lay_w(3, H, N, act_copy)
+        lay_w(3, 0, S3, dve_copy)
+        lay_w(3, S3, N, act_copy)
         quant_w(2, H, N)
         quant_w(3, 0, H)
         mx_rows([0, 1, 2], 1, [2])
         mx_rows([0, 1, 2], 0, [3])
-        lay_w(4, 0, H, dve_copy)
-        lay_w(4, H, N, act_copy)
+        lay_w(4, 0, S4, dve_copy)
+        lay_w(4, S4, N, act_copy)
         turn_o(6)
         turn_o(7)
         quant_w(3, H, N)
@@ -362,15 +372,15 @@ def tile_wind_farm_wakes_s2_kernel(tc, thrust, area, kern, outer, okern, inflow,
         turn_o(11)
         turn_t(7)
         speed_v(3)
-        lay_o(10, act_copy)
+        lay_o(10, dve_copy)
         lay_o(9, dve_copy)
         mx_tile(5, EXT + OWN)
-        square_v(3)
         square_t(6)
-        power_v(3)
-        quant_o(9, 11)
-        mx_tile(6, EXT)
+        square_v(3)
         area_t(6)
+        quant_o(9, 11)
+        power_v(3)
+        mx_tile(6, EXT)
         root_d2(4, 0)
         root_d2(4, 1)
         speed_v(4)

@@ -30,12 +30,14 @@ AREA_AT = {2: 5, 4: 6, 5: 7}
 MX_AT = {2: 5, 4: 6, 5: 7}
 S0 = 704
 WL = 7
-RB = 5
+RB = 4
 OUT_SLOTS = ["lay_w0", "lay_w1", "raw_w2_0", "raw_w3_0", "raw_w4_0", "lay_w2", "lay_w3", "lay_w4"]
-S1 = 576
+S1 = 544
 S2 = 512
 S3 = 512
-S4 = 640
+S4 = 576
+G0 = 832
+SHIFT = 32
 OWN = [0, 1]
 EXT = [2, 3, 4]
 
@@ -52,7 +54,6 @@ def tile_wind_farm_wakes_s2_kernel(tc, thrust, area, kern, outer, okern, inflow,
         inflow_f = keep.tile([P, ROWS], BF16, name="inflow_f")
         dummy = keep.tile([P, 1], F32, name="dummy")
         nc.gpsimd.memset(dummy[:], 1.0)
-        nc.scalar.activation(out=dummy[:], in_=dummy[:], func=ACT.Sqrt)
         ident = keep.tile([P, P], F32, name="ident")
         make_identity(nc, ident[:])
 
@@ -83,8 +84,8 @@ def tile_wind_farm_wakes_s2_kernel(tc, thrust, area, kern, outer, okern, inflow,
             for r in range(r0, r1):
                 o_raw[r] = raw[:, r - r0, :]
 
-        w_codes = [keep.tile([P, N], U32, name="w_codes_%d" % w, align_bytes=64) for w in range(NW)]
-        w_scales = [keep.tile([P, N], U8, name="w_scales_%d" % w, align_bytes=64) for w in range(NW)]
+        w_codes = [keep.tile([P, N], U32, name="w_codes_%d" % w, align_bytes=256) for w in range(NW)]
+        w_scales = [keep.tile([P, N], U8, name="w_scales_%d" % w, align_bytes=256) for w in range(NW)]
         w_lay = {}
 
         def lay_w(w, c0, c1, copy):
@@ -102,10 +103,10 @@ def tile_wind_farm_wakes_s2_kernel(tc, thrust, area, kern, outer, okern, inflow,
                 in_=w_lay[w][:, c0:c1].rearrange("p c j -> p (c j)"),
             )
 
-        a_codes = keep.tile([P, ROWS * GT * P], U32, name="a_codes", align_bytes=64)
-        a_scales = keep.tile([P, ROWS * GT * P], U8, name="a_scales", align_bytes=64)
-        o_codes = keep.tile([P, ROWS * GL * P], U32, name="o_codes", align_bytes=64)
-        o_scales = keep.tile([P, ROWS * GL * P], U8, name="o_scales", align_bytes=64)
+        a_codes = keep.tile([P, SHIFT + ROWS * GT * P], U32, name="a_codes", align_bytes=256)[:, SHIFT:]
+        a_scales = keep.tile([P, ROWS * GT * P], U8, name="a_scales", align_bytes=256)
+        o_codes = keep.tile([P, SHIFT + ROWS * GL * P], U32, name="o_codes", align_bytes=256)[:, SHIFT:]
+        o_scales = keep.tile([P, ROWS * GL * P], U8, name="o_scales", align_bytes=256)
 
         banks = {}
         held = {}
@@ -244,13 +245,13 @@ def tile_wind_farm_wakes_s2_kernel(tc, thrust, area, kern, outer, okern, inflow,
         act_copy = nc.scalar.copy
         dve_copy = nc.vector.tensor_copy
 
+        nc.scalar.dma_start(out=area_b[:], in_=area.rearrange("(g p j) -> p g j", g=GT, j=4))
+        nc.scalar.activation(out=dummy[:], in_=dummy[:], func=ACT.Sqrt)
         load_t(0, 1)
         load_t(1, 2)
         load_w(0, 0, Q)
-        nc.sync.dma_start(out=area_b[:], in_=area.rearrange("(g p j) -> p g j", g=GT, j=4))
         load_t(2, 3)
         load_t(3, 4)
-        nc.sync.dma_start(out=inflow_f[:], in_=inflow.rearrange("(p t) -> p t", t=ROWS))
         load_w(0, Q, N)
         load_t(4, 6)
         load_o(0, 2)
@@ -339,6 +340,7 @@ def tile_wind_farm_wakes_s2_kernel(tc, thrust, area, kern, outer, okern, inflow,
         mx_rows([0, 1], 1, [4])
         mx(2, 1, [3, 4])
         area_t(4)
+        nc.sync.dma_start(out=inflow_f[:], in_=inflow.rearrange("(p t) -> p t", t=ROWS))
         root_d2(0, 0)
         root_d2(1, 0)
         turn_o(8)

@@ -16,30 +16,22 @@ ACT = mybir.ActivationFunctionType
 ALU = mybir.AluOpType
 
 P = 128
-KP = 512
-GT = T // KP
-GL = L // KP
-NW = GT + GL
-ROWS = M // P
-PAIRS = ROWS // 2
-H = 512
-Q = 256
-LATE = 5
-EXT_FIRST = 4
-AREA_AT = {2: 5, 4: 6, 5: 7}
-MX_AT = {2: 5, 4: 6, 5: 7}
-S0 = 704
-WL = 7
-RB = 4
-OUT_SLOTS = ["lay_w0", "lay_w1", "raw_w2_0", "raw_w3_0", "raw_w4_0", "lay_w2", "lay_w3", "lay_w4"]
-S1 = 544
-S2 = 512
-S3 = 512
-S4 = 576
-G0 = 832
-SHIFT = 32
-OWN = [0, 1]
-EXT = [2, 3, 4]
+PASS = 512
+T_PASSES = T // PASS
+L_PASSES = L // PASS
+PASSES = T_PASSES + L_PASSES
+KERN = list(range(T_PASSES))
+OKERN = list(range(T_PASSES, PASSES))
+TILES = M // P
+HALF = 512
+BANKS = 8
+OUTER_BANKS = TILES * L_PASSES // 2
+VECTOR_COLUMNS = [608, 576, 512, 512, 576]
+OKERN_FIRST_FROM = 4
+STAGGER = 32
+SQUARES = 6
+ROOTS = 4
+RESULT_BUFFERS = ["laid_w0", "laid_w1", "raw_w2", "raw_w3", "raw_w4", "laid_w2", "laid_w3", "laid_w4"]
 
 
 def tile_wind_farm_wakes_s2_kernel(tc, thrust, area, kern, outer, okern, inflow, speed, power):
@@ -50,67 +42,71 @@ def tile_wind_farm_wakes_s2_kernel(tc, thrust, area, kern, outer, okern, inflow,
         psum = ctx.enter_context(tc.psum_pool(name="psum", bufs=1))
         ctx.enter_context(tc.manual_schedule())
 
-        area_b = keep.tile([P, GT, 4], BF16, name="area_b")
-        inflow_f = keep.tile([P, ROWS], BF16, name="inflow_f")
-        dummy = keep.tile([P, 1], F32, name="dummy")
-        nc.gpsimd.memset(dummy[:], 1.0)
+        area_k = keep.tile([P, T_PASSES, 4], BF16, name="area_k")
+        inflow_m = keep.tile([P, TILES], BF16, name="inflow_m")
+        warm = keep.tile([P, 1], F32, name="warm")
+        nc.gpsimd.memset(warm[:], 1.0)
         ident = keep.tile([P, P], F32, name="ident")
         make_identity(nc, ident[:])
 
-        w_hbm = [kern[g * KP:(g + 1) * KP, :] for g in range(GT)] + [okern[g * KP:(g + 1) * KP, :] for g in range(GL)]
-        thrust_rows = thrust.rearrange("(p t) k -> p t k", t=ROWS)
-        outer_rows = outer.rearrange("(p t) k -> p t k", t=ROWS)
-        speed_rows = speed.rearrange("(p t) n -> p t n", t=ROWS)
-        power_rows = power.rearrange("(p t) n -> p t n", t=ROWS)
+        weights = [kern[g * PASS:(g + 1) * PASS, :] for g in range(T_PASSES)]
+        weights = weights + [okern[g * PASS:(g + 1) * PASS, :] for g in range(L_PASSES)]
+        thrust_rows = thrust.rearrange("(p r) k -> p r k", r=TILES)
+        outer_rows = outer.rearrange("(p r) k -> p r k", r=TILES)
+        speed_rows = speed.rearrange("(p r) n -> p r n", r=TILES)
+        power_rows = power.rearrange("(p r) n -> p r n", r=TILES)
+
         w_raw = {}
-        t_raw = {}
-        o_raw = {}
+        thrust_raw = {}
+        outer_raw = {}
 
-        def load_w(w, c0, c1):
-            raw = keep.tile([P, 4, c1 - c0], BF16, name="raw_w%d_%d" % (w, c0), align_bytes=64)
-            nc.sync.dma_start(out=raw[:], in_=w_hbm[w].rearrange("(p j) n -> p j n", j=4)[:, :, c0:c1])
-            for c in range(c0, c1, 32):
-                w_raw[w, c] = raw[:, :, c - c0:]
+        def load_weights(w):
+            w_raw[w] = keep.tile([P, 4, N], BF16, name="raw_w%d" % w, align_bytes=64)
+            nc.sync.dma_start(out=w_raw[w][:], in_=weights[w].rearrange("(p t) n -> p t n", t=4))
 
-        def load_t(r0, r1, slot=None):
-            raw = keep.tile([P, r1 - r0, T], BF16, name=slot or "raw_t%d" % r0, align_bytes=64)
+        def load_thrust(r0, r1, buffer=None):
+            raw = keep.tile([P, r1 - r0, T], BF16, name=buffer or "raw_thrust%d" % r0, align_bytes=64)
             nc.sync.dma_start(out=raw[:], in_=thrust_rows[:, r0:r1, :])
             for r in range(r0, r1):
-                t_raw[r] = raw[:, r - r0, :]
+                thrust_raw[r] = raw[:, r - r0, :]
 
-        def load_o(r0, r1, slot=None):
-            raw = keep.tile([P, r1 - r0, L], BF16, name=slot or "raw_o%d" % r0, align_bytes=64)
+        def load_outer(r0, r1, buffer=None):
+            raw = keep.tile([P, r1 - r0, L], BF16, name=buffer or "raw_outer%d" % r0, align_bytes=64)
             nc.sync.dma_start(out=raw[:], in_=outer_rows[:, r0:r1, :])
             for r in range(r0, r1):
-                o_raw[r] = raw[:, r - r0, :]
+                outer_raw[r] = raw[:, r - r0, :]
 
-        w_codes = [keep.tile([P, N], U32, name="w_codes_%d" % w, align_bytes=256) for w in range(NW)]
-        w_scales = [keep.tile([P, N], U8, name="w_scales_%d" % w, align_bytes=256) for w in range(NW)]
-        w_lay = {}
+        w_codes = [keep.tile([P, N], U32, name="w_codes_%d" % w, align_bytes=256) for w in range(PASSES)]
+        w_scales = [keep.tile([P, N], U8, name="w_scales_%d" % w, align_bytes=256) for w in range(PASSES)]
+        w_laid = {}
 
-        def lay_w(w, c0, c1, copy):
-            if w not in w_lay:
-                w_lay[w] = keep.tile([P, N, 4], BF16, name="lay_w%d" % w, align_bytes=64)
+        def lay_weights(w, c0, c1, copy):
+            if w not in w_laid:
+                w_laid[w] = keep.tile([P, N, 4], BF16, name="laid_w%d" % w, align_bytes=64)
             copy(
-                out=w_lay[w][:, c0:c1].rearrange("p (c i) j -> p c j i", i=4),
-                in_=w_raw[w, c0][:, :, 0:c1 - c0].rearrange("p j (c i) -> p c j i", i=4),
+                out=w_laid[w][:, c0:c1].rearrange("p (c i) t -> p c t i", i=4),
+                in_=w_raw[w][:, :, c0:c1].rearrange("p t (c i) -> p c t i", i=4),
             )
 
-        def quant_w(w, c0, c1):
+        def lay_weights_both(w):
+            lay_weights(w, 0, VECTOR_COLUMNS[w], nc.vector.tensor_copy)
+            lay_weights(w, VECTOR_COLUMNS[w], N, nc.scalar.copy)
+
+        def quantise_weights(w, c0, c1):
             nc.vector.quantize_mx(
                 out=w_codes[w][:, c0:c1].bitcast(E4M3),
                 scales=w_scales[w][:, c0:c1],
-                in_=w_lay[w][:, c0:c1].rearrange("p c j -> p (c j)"),
+                in_=w_laid[w][:, c0:c1].rearrange("p c t -> p (c t)"),
             )
 
-        a_codes = keep.tile([P, SHIFT + ROWS * GT * P], U32, name="a_codes", align_bytes=256)[:, SHIFT:]
-        a_scales = keep.tile([P, ROWS * GT * P], U8, name="a_scales", align_bytes=256)
-        o_codes = keep.tile([P, SHIFT + ROWS * GL * P], U32, name="o_codes", align_bytes=256)[:, SHIFT:]
-        o_scales = keep.tile([P, ROWS * GL * P], U8, name="o_scales", align_bytes=256)
+        a_codes = keep.tile([P, STAGGER + TILES * T_PASSES * P], U32, name="a_codes", align_bytes=256)[:, STAGGER:]
+        a_scales = keep.tile([P, TILES * T_PASSES * P], U8, name="a_scales", align_bytes=256)
+        o_codes = keep.tile([P, STAGGER + TILES * L_PASSES * P], U32, name="o_codes", align_bytes=256)[:, STAGGER:]
+        o_scales = keep.tile([P, TILES * L_PASSES * P], U8, name="o_scales", align_bytes=256)
 
         banks = {}
         held = {}
-        empty = list(range(8))
+        empty = list(range(BANKS))
 
         def take_bank(key, shape):
             held[key] = empty.pop(0)
@@ -120,70 +116,70 @@ def tile_wind_farm_wakes_s2_kernel(tc, thrust, area, kern, outer, okern, inflow,
         def give_bank(key):
             empty.append(held.pop(key))
 
-        def turn_units(key, units):
+        def turn(key, units):
             bank = take_bank(key, [P, 2, 2 * P])
             for s, (raw, g) in enumerate(units):
                 words = raw.bitcast(F32)
                 for u in range(2):
                     nc.tensor.transpose(bank[:, u, s * P:(s + 1) * P], words[:, 256 * g + u:256 * (g + 1):2], ident[:])
 
-        def turn_t(r):
-            turn_units(("t", r), [(t_raw[r], g) for g in range(GT)])
+        def turn_thrust(r):
+            turn(("thrust", r), [(thrust_raw[r], g) for g in range(T_PASSES)])
 
-        def turn_o(b):
-            turn_units(("o", b), [(o_raw[s // GL], s % GL) for s in (2 * b, 2 * b + 1)])
+        def turn_outer(b):
+            turn(("outer", b), [(outer_raw[s // L_PASSES], s % L_PASSES) for s in (2 * b, 2 * b + 1)])
 
-        t_sq = {}
-        t_a = {}
-        o_lay = keep.tile([P, ROWS * GL // 2, 2 * P, 2], F32, name="o_lay", align_bytes=64)
+        thrust_sq = {}
+        a_pair = {}
+        outer_laid = keep.tile([P, OUTER_BANKS, 2 * P, 2], F32, name="outer_laid", align_bytes=64)
 
-        def square_t(r):
-            t_sq[r] = work.tile([P, 2 * P, 4], F32, name="t_sq", bufs=6, align_bytes=64)
+        def square_thrust(r):
+            thrust_sq[r] = work.tile([P, 2 * P, 4], F32, name="square", bufs=SQUARES, align_bytes=64)
             nc.scalar.activation(
-                out=t_sq[r][:].rearrange("p c (u e) -> p c u e", e=2),
-                in_=banks["t", r][:].bitcast(BF16).rearrange("p u (c e) -> p c u e", e=2),
+                out=thrust_sq[r][:].rearrange("p c (u e) -> p c u e", e=2),
+                in_=banks["thrust", r][:].bitcast(BF16).rearrange("p u (c e) -> p c u e", e=2),
                 func=ACT.Square,
             )
-            give_bank(("t", r))
+            give_bank(("thrust", r))
 
-        def area_t(r):
+        def times_area(r):
             if r % 2 == 0:
-                t_a[r // 2] = work.tile([P, 2, GT, P, 4], BF16, name="t_a", bufs=2, align_bytes=64)
+                a_pair[r // 2] = work.tile([P, 2, T_PASSES, P, 4], BF16, name="a_pair", bufs=2, align_bytes=64)
             nc.vector.tensor_tensor(
-                out=t_a[r // 2][:, r % 2],
-                in0=t_sq[r][:].rearrange("p (g c) j -> p g c j", g=GT),
-                in1=area_b[:].unsqueeze(2).to_broadcast([P, GT, P, 4]),
+                out=a_pair[r // 2][:, r % 2],
+                in0=thrust_sq[r][:].rearrange("p (g c) t -> p g c t", g=T_PASSES),
+                in1=area_k[:].unsqueeze(2).to_broadcast([P, T_PASSES, P, 4]),
                 op=ALU.mult,
             )
 
-        def quant_t(r0, r1):
-            cols = slice(r0 * GT * P, r1 * GT * P)
+        def quantise_a(r0, r1):
+            cols = slice(r0 * T_PASSES * P, r1 * T_PASSES * P)
             nc.vector.quantize_mx(
                 out=a_codes[:, cols].bitcast(E5M2),
                 scales=a_scales[:, cols],
-                in_=t_a[r0 // 2][:, r0 % 2:r0 % 2 + r1 - r0].rearrange("p r g c j -> p (r g c j)"),
+                in_=a_pair[r0 // 2][:, r0 % 2:r0 % 2 + r1 - r0].rearrange("p r g c t -> p (r g c t)"),
             )
 
-        def lay_o(b, copy):
-            copy(out=o_lay[:, b], in_=banks["o", b][:].rearrange("p u c -> p c u"))
-            give_bank(("o", b))
+        def lay_outer(b, copy=nc.scalar.copy):
+            copy(out=outer_laid[:, b], in_=banks["outer", b][:].rearrange("p u c -> p c u"))
+            give_bank(("outer", b))
 
-        def quant_o(b0, b1):
+        def quantise_outer(b0, b1):
             cols = slice(b0 * 2 * P, b1 * 2 * P)
-            src = o_lay[:, b0:b1].rearrange("p g c u -> p (g c u)").bitcast(BF16)
-            nc.vector.quantize_mx(out=o_codes[:, cols].bitcast(E4M3), scales=o_scales[:, cols], in_=src)
+            values = outer_laid[:, b0:b1].rearrange("p b c u -> p (b c u)").bitcast(BF16)
+            nc.vector.quantize_mx(out=o_codes[:, cols].bitcast(E4M3), scales=o_scales[:, cols], in_=values)
 
-        def mx(r, h, passes):
+        def add_passes(r, h, passes):
             if (r, h) not in banks:
-                take_bank((r, h), [P, H])
-            cols = slice(h * H, (h + 1) * H)
-            order = OWN + EXT if r < EXT_FIRST else EXT + OWN
+                take_bank((r, h), [P, HALF])
+            cols = slice(h * HALF, (h + 1) * HALF)
+            order = KERN + OKERN if r < OKERN_FIRST_FROM else OKERN + KERN
             for w in passes:
-                if w < GT:
-                    rows = slice((r * GT + w) * P, (r * GT + w + 1) * P)
+                if w in KERN:
+                    rows = slice((r * T_PASSES + w) * P, (r * T_PASSES + w + 1) * P)
                     codes, scales = a_codes[:, rows].bitcast(E5M2), a_scales[:, rows]
                 else:
-                    rows = slice((r * GL + w - GT) * P, (r * GL + w - GT + 1) * P)
+                    rows = slice((r * L_PASSES + w - T_PASSES) * P, (r * L_PASSES + w - T_PASSES + 1) * P)
                     codes, scales = o_codes[:, rows].bitcast(E4M3), o_scales[:, rows]
                 nc.tensor.matmul_mx(
                     out=banks[r, h][:],
@@ -195,222 +191,213 @@ def tile_wind_farm_wakes_s2_kernel(tc, thrust, area, kern, outer, okern, inflow,
                     stop=(w == order[-1]),
                 )
 
-        spare = []
+        def add_pass_to_tiles(w, h, tiles):
+            for r in tiles:
+                add_passes(r, h, [w])
 
-        def out_tile(k):
-            if not spare:
-                both = keep.tile([P, 2, N], F32, name=OUT_SLOTS[(len(vel) + len(pw)) // 2], align_bytes=64)
-                spare.append(both[:, 1, :])
-                return both[:, 0, :]
-            return spare.pop()
+        def add_to_tile(r, passes):
+            for h in range(2):
+                add_passes(r, h, passes)
 
         root = {}
-        vel = {}
-        vel2 = {}
-        pw = {}
+        speed_sb = {}
+        speed_sq = {}
+        power_sb = {}
+        second_half = []
 
-        def root_d2(r, h):
+        def result_tile():
+            if second_half:
+                return second_half.pop()
+            name = RESULT_BUFFERS[(len(speed_sb) + len(power_sb)) // 2]
+            both = keep.tile([P, 2, N], F32, name=name, align_bytes=64)
+            second_half.append(both[:, 1, :])
+            return both[:, 0, :]
+
+        def take_root(r, h):
             if r not in root:
-                root[r] = work.tile([P, N], F32, name="root", bufs=RB)
-            nc.scalar.activation(out=root[r][:, h * H:(h + 1) * H], in_=banks[r, h][:], func=ACT.Sqrt)
+                root[r] = work.tile([P, N], F32, name="root", bufs=ROOTS)
+            nc.scalar.activation(out=root[r][:, h * HALF:(h + 1) * HALF], in_=banks[r, h][:], func=ACT.Sqrt)
             give_bank((r, h))
 
-        def square_v(r, c0=0, c1=N):
-            if r not in vel2:
-                vel2[r] = work.tile([P, N], F32, name="t_sq", bufs=6, align_bytes=64)
+        def take_roots(r):
+            for h in range(2):
+                take_root(r, h)
+
+        def square_speed(r, c0=0, c1=N):
+            if r not in speed_sq:
+                speed_sq[r] = work.tile([P, N], F32, name="square", bufs=SQUARES, align_bytes=64)
             nc.scalar.activation(
-                out=vel2[r][:, c0:c1], in_=root[r][:, c0:c1], func=ACT.Square, scale=-1.0, bias=inflow_f[:, r:r + 1]
+                out=speed_sq[r][:, c0:c1], in_=root[r][:, c0:c1], func=ACT.Square, scale=-1.0, bias=inflow_m[:, r:r + 1]
             )
 
-        def square_v_dve(r, c0, c1):
-            if r not in vel2:
-                vel2[r] = work.tile([P, N], F32, name="t_sq", bufs=6, align_bytes=64)
-            nc.vector.tensor_tensor(out=vel2[r][:, c0:c1], in0=vel[r][:, c0:c1], in1=vel[r][:, c0:c1], op=ALU.mult)
-
-        def speed_v(r, c0=0, c1=N):
-            if r not in vel:
-                vel[r] = out_tile(2 * r)
+        def store_speed(r):
+            speed_sb[r] = result_tile()
             nc.vector.tensor_scalar(
-                out=vel[r][:, c0:c1], in0=root[r][:, c0:c1], scalar1=-1.0, scalar2=inflow_f[:, r:r + 1],
+                out=speed_sb[r][:, 0:N], in0=root[r][:, 0:N], scalar1=-1.0, scalar2=inflow_m[:, r:r + 1],
                 op0=ALU.mult, op1=ALU.add,
             )
-            nc.sync.dma_start(out=speed_rows[:, r, c0:c1], in_=vel[r][:, c0:c1])
+            nc.sync.dma_start(out=speed_rows[:, r, 0:N], in_=speed_sb[r][:, 0:N])
 
-        def power_v(r, c0=0, c1=N):
-            if r not in pw:
-                pw[r] = out_tile(2 * r + 1)
-            nc.vector.tensor_tensor(out=pw[r][:, c0:c1], in0=vel2[r][:, c0:c1], in1=vel[r][:, c0:c1], op=ALU.mult)
-            nc.sync.dma_start(out=power_rows[:, r, c0:c1], in_=pw[r][:, c0:c1])
+        def store_power(r, c0=0, c1=N):
+            if r not in power_sb:
+                power_sb[r] = result_tile()
+            nc.vector.tensor_tensor(
+                out=power_sb[r][:, c0:c1], in0=speed_sq[r][:, c0:c1], in1=speed_sb[r][:, c0:c1], op=ALU.mult
+            )
+            nc.sync.dma_start(out=power_rows[:, r, c0:c1], in_=power_sb[r][:, c0:c1])
 
-        act_copy = nc.scalar.copy
-        dve_copy = nc.vector.tensor_copy
+        nc.scalar.dma_start(out=area_k[:], in_=area.rearrange("(g p t) -> p g t", g=T_PASSES, t=4))
+        nc.scalar.activation(out=warm[:], in_=warm[:], func=ACT.Sqrt)
 
-        nc.scalar.dma_start(out=area_b[:], in_=area.rearrange("(g p j) -> p g j", g=GT, j=4))
-        nc.scalar.activation(out=dummy[:], in_=dummy[:], func=ACT.Sqrt)
-        load_t(0, 1)
-        load_t(1, 2)
-        load_w(0, 0, Q)
-        load_t(2, 3)
-        load_t(3, 4)
-        load_w(0, Q, N)
-        load_t(4, 6)
-        load_o(0, 2)
-        load_w(1, 0, N)
-        load_o(2, 4)
-        load_w(2, 0, N)
-        load_w(3, 0, N)
-        load_w(4, 0, N)
-        load_o(4, 6)
-
-        def mx_rows(rows, h, passes):
-            for w in passes:
-                for r in rows:
-                    mx(r, h, [w])
-
-        def mx_tile(r, passes):
-            for h in range(2):
-                mx(r, h, passes)
+        load_thrust(0, 1)
+        load_thrust(1, 2)
+        load_thrust(2, 4)
+        load_weights(0)
+        load_thrust(4, 6)
+        load_outer(0, 2)
+        load_weights(1)
+        load_outer(2, 4)
+        for w in OKERN:
+            load_weights(w)
+        load_outer(4, 6)
 
         for r in range(4):
-            turn_t(r)
-        square_t(0)
-        lay_w(0, 0, Q, dve_copy)
-        quant_w(0, 0, Q)
-        square_t(1)
-        area_t(0)
-        square_t(2)
-        area_t(1)
-        square_t(3)
-        lay_w(0, Q, S0, dve_copy)
-        quant_t(0, 2)
-        lay_w(0, S0, N, act_copy)
-        load_t(6, 8, "raw_w0_256")
-        turn_t(4)
-        turn_t(5)
-        area_t(2)
-        square_t(4)
-        quant_w(0, Q, H)
-        area_t(3)
-        quant_w(0, H, N)
-        square_t(5)
-        for b in range(3):
-            turn_o(b)
-        mx_rows([0, 1], 0, [0])
-        mx_rows([0, 1], 1, [0])
-        quant_t(2, 4)
-        for b in range(3):
-            lay_o(b, act_copy)
-        lay_w(1, 0, S1, dve_copy)
-        lay_w(1, S1, N, act_copy)
-        load_o(6, 8, "raw_w1_0")
-        quant_o(0, 2)
-        quant_w(1, 0, H)
+            turn_thrust(r)
+        square_thrust(0)
+        square_thrust(1)
+        times_area(0)
+        square_thrust(2)
+        times_area(1)
+        square_thrust(3)
+        lay_weights(0, 0, VECTOR_COLUMNS[0], nc.vector.tensor_copy)
+        quantise_a(0, 2)
+        lay_weights(0, VECTOR_COLUMNS[0], N, nc.scalar.copy)
+        load_thrust(6, 8, "raw_w0")
+        turn_thrust(4)
+        turn_thrust(5)
+        times_area(2)
+        square_thrust(4)
+        quantise_weights(0, 0, HALF)
+        times_area(3)
+        quantise_weights(0, HALF, N)
+        square_thrust(5)
+
+        for b in range(0, 3):
+            turn_outer(b)
+        for h in range(2):
+            add_pass_to_tiles(0, h, [0, 1])
+        quantise_a(2, 4)
+        for b in range(0, 3):
+            lay_outer(b)
+        lay_weights_both(1)
+        load_outer(6, 8, "raw_w1")
+        quantise_outer(0, 2)
+        quantise_weights(1, 0, HALF)
         for b in range(3, 6):
-            turn_o(b)
-        mx_rows([0, 1], 0, [1])
-        quant_o(2, 3)
-        quant_w(1, H, N)
-        mx_rows([0, 1], 1, [1])
+            turn_outer(b)
+        add_pass_to_tiles(1, 0, [0, 1])
+        quantise_outer(2, 3)
+        quantise_weights(1, HALF, N)
+        add_pass_to_tiles(1, 1, [0, 1])
         for b in range(3, 6):
-            lay_o(b, act_copy)
-        mx_tile(2, OWN)
-        lay_w(2, 0, S2, dve_copy)
-        lay_w(2, S2, N, act_copy)
-        quant_o(3, 5)
-        quant_w(2, 0, H)
-        mx_rows([0, 1, 2], 0, [2])
-        lay_w(3, 0, S3, dve_copy)
-        lay_w(3, S3, N, act_copy)
-        quant_w(2, H, N)
-        quant_w(3, 0, H)
-        mx_rows([0, 1, 2], 1, [2])
-        mx_rows([0, 1, 2], 0, [3])
-        lay_w(4, 0, S4, dve_copy)
-        lay_w(4, S4, N, act_copy)
-        turn_o(6)
-        turn_o(7)
-        quant_w(3, H, N)
-        quant_w(4, 0, H)
-        mx_rows([0, 1], 1, [3])
-        mx_rows([0, 1, 2], 0, [4])
-        quant_o(5, 6)
-        lay_o(6, act_copy)
-        lay_o(7, act_copy)
-        quant_w(4, H, N)
-        mx_rows([0, 1], 1, [4])
-        mx(2, 1, [3, 4])
-        area_t(4)
-        nc.sync.dma_start(out=inflow_f[:], in_=inflow.rearrange("(p t) -> p t", t=ROWS))
-        root_d2(0, 0)
-        root_d2(1, 0)
-        turn_o(8)
-        root_d2(0, 1)
-        mx_tile(3, range(NW))
-        quant_o(6, 8)
-        quant_t(4, 5)
-        root_d2(1, 1)
-        speed_v(0)
-        square_v(0)
-        speed_v(1)
-        area_t(5)
-        square_v(1)
-        mx(4, 0, EXT + OWN)
-        root_d2(2, 0)
-        root_d2(2, 1)
-        power_v(0)
-        quant_t(5, 6)
-        lay_o(8, act_copy)
-        turn_o(9)
-        turn_o(10)
-        turn_t(6)
-        mx(4, 1, EXT + OWN)
-        power_v(1)
-        speed_v(2)
-        quant_o(8, 9)
-        square_v(2)
-        power_v(2)
-        root_d2(3, 0)
-        root_d2(3, 1)
-        turn_o(11)
-        turn_t(7)
-        speed_v(3)
-        lay_o(10, dve_copy)
-        lay_o(9, dve_copy)
-        mx_tile(5, EXT + OWN)
-        square_t(6)
-        square_v(3)
-        area_t(6)
-        quant_o(9, 11)
-        power_v(3)
-        mx_tile(6, EXT)
-        root_d2(4, 0)
-        root_d2(4, 1)
-        speed_v(4)
-        quant_t(6, 7)
-        mx_tile(6, OWN)
-        lay_o(11, act_copy)
-        square_v(4)
-        square_t(7)
-        power_v(4)
-        quant_o(11, 12)
-        mx_tile(7, EXT)
-        area_t(7)
-        root_d2(5, 0)
-        root_d2(5, 1)
-        speed_v(5)
-        quant_t(7, 8)
-        mx_tile(7, OWN)
-        root_d2(6, 0)
-        root_d2(6, 1)
-        square_v(5)
-        speed_v(6)
-        power_v(5)
-        square_v(6)
-        power_v(6)
-        root_d2(7, 0)
-        root_d2(7, 1)
-        speed_v(7)
-        square_v(7, 0, H)
-        square_v(7, H, N)
-        power_v(7, 0, H)
-        power_v(7, H, N)
+            lay_outer(b)
+        add_to_tile(2, KERN)
+
+        early = [0, 1, 2]
+        lay_weights_both(2)
+        quantise_outer(3, 5)
+        quantise_weights(2, 0, HALF)
+        add_pass_to_tiles(2, 0, early)
+        lay_weights_both(3)
+        quantise_weights(2, HALF, N)
+        quantise_weights(3, 0, HALF)
+        add_pass_to_tiles(2, 1, early)
+        add_pass_to_tiles(3, 0, early)
+        lay_weights_both(4)
+        turn_outer(6)
+        turn_outer(7)
+        quantise_weights(3, HALF, N)
+        quantise_weights(4, 0, HALF)
+        add_pass_to_tiles(3, 1, [0, 1])
+        add_pass_to_tiles(4, 0, early)
+        quantise_outer(5, 6)
+        lay_outer(6)
+        lay_outer(7)
+        quantise_weights(4, HALF, N)
+        add_pass_to_tiles(4, 1, [0, 1])
+        add_passes(2, 1, [3, 4])
+
+        times_area(4)
+        nc.sync.dma_start(out=inflow_m[:], in_=inflow.rearrange("(p r) -> p r", r=TILES))
+        take_root(0, 0)
+        take_root(1, 0)
+        turn_outer(8)
+        take_root(0, 1)
+        add_to_tile(3, KERN + OKERN)
+        quantise_outer(6, 8)
+        quantise_a(4, 5)
+        take_root(1, 1)
+        store_speed(0)
+        square_speed(0)
+        store_speed(1)
+        times_area(5)
+        square_speed(1)
+        add_passes(4, 0, OKERN + KERN)
+
+        take_roots(2)
+        store_power(0)
+        quantise_a(5, 6)
+        lay_outer(8)
+        turn_outer(9)
+        turn_outer(10)
+        turn_thrust(6)
+        add_passes(4, 1, OKERN + KERN)
+        store_power(1)
+        store_speed(2)
+        quantise_outer(8, 9)
+        square_speed(2)
+        store_power(2)
+
+        take_roots(3)
+        turn_outer(11)
+        turn_thrust(7)
+        store_speed(3)
+        lay_outer(10, nc.vector.tensor_copy)
+        lay_outer(9, nc.vector.tensor_copy)
+        add_to_tile(5, OKERN + KERN)
+        square_thrust(6)
+        square_speed(3)
+        times_area(6)
+        quantise_outer(9, 11)
+        store_power(3)
+        add_to_tile(6, OKERN)
+
+        take_roots(4)
+        store_speed(4)
+        quantise_a(6, 7)
+        add_to_tile(6, KERN)
+        lay_outer(11)
+        square_speed(4)
+        square_thrust(7)
+        store_power(4)
+        quantise_outer(11, 12)
+        add_to_tile(7, OKERN)
+        times_area(7)
+
+        take_roots(5)
+        store_speed(5)
+        quantise_a(7, 8)
+        add_to_tile(7, KERN)
+        take_roots(6)
+        square_speed(5)
+        store_speed(6)
+        store_power(5)
+        square_speed(6)
+        store_power(6)
+
+        take_roots(7)
+        store_speed(7)
+        for h in range(2):
+            square_speed(7, h * HALF, (h + 1) * HALF)
+        for h in range(2):
+            store_power(7, h * HALF, (h + 1) * HALF)

@@ -84,8 +84,8 @@ def tile_wind_farm_wakes_s2_kernel(tc, thrust, area, kern, outer, okern, inflow,
             if w not in w_laid:
                 w_laid[w] = keep.tile([P, N, 4], BF16, name="laid_w%d" % w, align_bytes=64)
             copy(
-                out=w_laid[w][:, c0:c1].rearrange("p (c i) t -> p c t i", i=4),
-                in_=w_raw[w][:, :, c0:c1].rearrange("p t (c i) -> p c t i", i=4),
+                out=w_laid[w][:, c0:c1].rearrange("p (c i) t -> p c t i", i=8),
+                in_=w_raw[w][:, :, c0:c1].rearrange("p t (c i) -> p c t i", i=8),
             )
 
         def lay_weights_both(w):

@@ -26,7 +26,7 @@ TILES = M // P
 HALF = 512
 BANKS = 8
 OUTER_BANKS = TILES * L_PASSES // 2
-VECTOR_COLUMNS = [608, 576, 512, 512, 576]
+VECTOR_COLUMNS = [608, 640, 512, 512, 640]
 OKERN_FIRST_FROM = 4
 STAGGER = 32
 SQUARES = 6
@@ -259,7 +259,9 @@ def tile_wind_farm_wakes_s2_kernel(tc, thrust, area, kern, outer, okern, inflow,
         load_outer(2, 4)
         for w in OKERN:
             load_weights(w)
-        load_outer(4, 6)
+        load_outer(4, 5)
+        load_outer(5, 6)
+        nc.sync.dma_start(out=inflow_m[:], in_=inflow.rearrange("(p r) -> p r", r=TILES))
 
         for r in range(4):
             turn_thrust(r)
@@ -328,7 +330,6 @@ def tile_wind_farm_wakes_s2_kernel(tc, thrust, area, kern, outer, okern, inflow,
         add_passes(2, 1, [3, 4])
 
         times_area(4)
-        nc.sync.dma_start(out=inflow_m[:], in_=inflow.rearrange("(p r) -> p r", r=TILES))
         take_root(0, 0)
         take_root(1, 0)
         turn_outer(8)
@@ -348,10 +349,10 @@ def tile_wind_farm_wakes_s2_kernel(tc, thrust, area, kern, outer, okern, inflow,
         store_power(0)
         quantise_a(5, 6)
         lay_outer(8)
-        turn_outer(9)
-        turn_outer(10)
         turn_thrust(6)
+        turn_outer(10)
         add_passes(4, 1, OKERN + KERN)
+        turn_outer(9)
         store_power(1)
         store_speed(2)
         quantise_outer(8, 9)

@@ -61,17 +61,17 @@ def tile_wind_farm_wakes_s2_kernel(tc, thrust, area, kern, outer, okern, inflow,
         outer_raw = {}
 
         def load_weights(w):
-            w_raw[w] = keep.tile([P, 4, N], BF16, name="raw_w%d" % w, align_bytes=64)
+            w_raw[w] = keep.tile([P, 4, N], BF16, name="raw_w%d" % w, align_bytes=256)
             nc.sync.dma_start(out=w_raw[w][:], in_=weights[w].rearrange("(p t) n -> p t n", t=4))
 
         def load_thrust(r0, r1, buffer=None):
-            raw = keep.tile([P, r1 - r0, T], BF16, name=buffer or "raw_thrust%d" % r0, align_bytes=64)
+            raw = keep.tile([P, r1 - r0, T], BF16, name=buffer or "raw_thrust%d" % r0, align_bytes=256)
             nc.sync.dma_start(out=raw[:], in_=thrust_rows[:, r0:r1, :])
             for r in range(r0, r1):
                 thrust_raw[r] = raw[:, r - r0, :]
 
         def load_outer(r0, r1, buffer=None):
-            raw = keep.tile([P, r1 - r0, L], BF16, name=buffer or "raw_outer%d" % r0, align_bytes=64)
+            raw = keep.tile([P, r1 - r0, L], BF16, name=buffer or "raw_outer%d" % r0, align_bytes=256)
             nc.sync.dma_start(out=raw[:], in_=outer_rows[:, r0:r1, :])
             for r in range(r0, r1):
                 outer_raw[r] = raw[:, r - r0, :]
@@ -82,7 +82,7 @@ def tile_wind_farm_wakes_s2_kernel(tc, thrust, area, kern, outer, okern, inflow,
 
         def lay_weights(w, c0, c1, copy):
             if w not in w_laid:
-                w_laid[w] = keep.tile([P, N, 4], BF16, name="laid_w%d" % w, align_bytes=64)
+                w_laid[w] = keep.tile([P, N, 4], BF16, name="laid_w%d" % w, align_bytes=256)
             copy(
                 out=w_laid[w][:, c0:c1].rearrange("p (c i) t -> p c t i", i=8),
                 in_=w_raw[w][:, :, c0:c1].rearrange("p t (c i) -> p c t i", i=8),
@@ -129,12 +129,13 @@ def tile_wind_farm_wakes_s2_kernel(tc, thrust, area, kern, outer, okern, inflow,
         def turn_outer(b):
             turn(("outer", b), [(outer_raw[s // L_PASSES], s % L_PASSES) for s in (2 * b, 2 * b + 1)])
 
+        area_rows = keep.tile([P, T_PASSES, P, 4], BF16, name="area_rows", align_bytes=256)
         thrust_sq = {}
         a_pair = {}
-        outer_laid = keep.tile([P, OUTER_BANKS, 2 * P, 2], F32, name="outer_laid", align_bytes=64)
+        outer_laid = keep.tile([P, OUTER_BANKS, 2 * P, 2], F32, name="outer_laid", align_bytes=256)
 
         def square_thrust(r):
-            thrust_sq[r] = work.tile([P, 2 * P, 4], F32, name="square", bufs=SQUARES, align_bytes=64)
+            thrust_sq[r] = work.tile([P, 2 * P, 4], F32, name="square", bufs=SQUARES, align_bytes=256)
             nc.scalar.activation(
                 out=thrust_sq[r][:].rearrange("p c (u e) -> p c u e", e=2),
                 in_=banks["thrust", r][:].bitcast(BF16).rearrange("p u (c e) -> p c u e", e=2),
@@ -144,11 +145,11 @@ def tile_wind_farm_wakes_s2_kernel(tc, thrust, area, kern, outer, okern, inflow,
 
         def times_area(r):
             if r % 2 == 0:
-                a_pair[r // 2] = work.tile([P, 2, T_PASSES, P, 4], BF16, name="a_pair", bufs=2, align_bytes=64)
+                a_pair[r // 2] = work.tile([P, 2, T_PASSES, P, 4], BF16, name="a_pair", bufs=2, align_bytes=256)
             nc.vector.tensor_tensor(
                 out=a_pair[r // 2][:, r % 2],
                 in0=thrust_sq[r][:].rearrange("p (g c) t -> p g c t", g=T_PASSES),
-                in1=area_k[:].unsqueeze(2).to_broadcast([P, T_PASSES, P, 4]),
+                in1=area_rows[:],
                 op=ALU.mult,
             )
 
@@ -209,7 +210,7 @@ def tile_wind_farm_wakes_s2_kernel(tc, thrust, area, kern, outer, okern, inflow,
             if second_half:
                 return second_half.pop()
             name = RESULT_BUFFERS[(len(speed_sb) + len(power_sb)) // 2]
-            both = keep.tile([P, 2, N], F32, name=name, align_bytes=64)
+            both = keep.tile([P, 2, N], F32, name=name, align_bytes=256)
             second_half.append(both[:, 1, :])
             return both[:, 0, :]
 
@@ -225,7 +226,7 @@ def tile_wind_farm_wakes_s2_kernel(tc, thrust, area, kern, outer, okern, inflow,
 
         def square_speed(r, c0=0, c1=N):
             if r not in speed_sq:
-                speed_sq[r] = work.tile([P, N], F32, name="square", bufs=SQUARES, align_bytes=64)
+                speed_sq[r] = work.tile([P, N], F32, name="square", bufs=SQUARES, align_bytes=256)
             nc.scalar.activation(
                 out=speed_sq[r][:, c0:c1], in_=root[r][:, c0:c1], func=ACT.Square, scale=-1.0, bias=inflow_m[:, r:r + 1]
             )
@@ -259,10 +260,11 @@ def tile_wind_farm_wakes_s2_kernel(tc, thrust, area, kern, outer, okern, inflow,
         load_outer(2, 4)
         for w in OKERN:
             load_weights(w)
-        load_outer(4, 5)
-        load_outer(5, 6)
+        load_outer(4, 5, "raw_thrust2")
+        load_outer(5, 6, "raw_thrust4")
         nc.sync.dma_start(out=inflow_m[:], in_=inflow.rearrange("(p r) -> p r", r=TILES))
 
+        nc.vector.tensor_copy(out=area_rows[:], in_=area_k[:].unsqueeze(2).to_broadcast([P, T_PASSES, P, 4]))
         for r in range(4):
             turn_thrust(r)
         square_thrust(0)

@@ -28,9 +28,12 @@ BANKS = 8
 OUTER_BANKS = TILES * L_PASSES // 2
 VECTOR_COLUMNS = [608, 640, 512, 512, 640]
 OKERN_FIRST_FROM = 4
+ALIGN = 256
 STAGGER = 32
+LINE = 8
 SQUARES = 6
 ROOTS = 4
+A_PAIRS = 2
 RESULT_BUFFERS = ["laid_w0", "laid_w1", "raw_w2", "raw_w3", "raw_w4", "laid_w2", "laid_w3", "laid_w4"]
 
 
@@ -38,7 +41,7 @@ def tile_wind_farm_wakes_s2_kernel(tc, thrust, area, kern, outer, okern, inflow,
     nc = tc.nc
     with ExitStack() as ctx:
         keep = ctx.enter_context(tc.tile_pool(name="keep", bufs=1))
-        work = ctx.enter_context(tc.tile_pool(name="work", bufs=2))
+        work = ctx.enter_context(tc.tile_pool(name="work", bufs=A_PAIRS))
         psum = ctx.enter_context(tc.psum_pool(name="psum", bufs=1))
         ctx.enter_context(tc.manual_schedule())
 
@@ -61,31 +64,31 @@ def tile_wind_farm_wakes_s2_kernel(tc, thrust, area, kern, outer, okern, inflow,
         outer_raw = {}
 
         def load_weights(w):
-            w_raw[w] = keep.tile([P, 4, N], BF16, name="raw_w%d" % w, align_bytes=256)
+            w_raw[w] = keep.tile([P, 4, N], BF16, name="raw_w%d" % w, align_bytes=ALIGN)
             nc.sync.dma_start(out=w_raw[w][:], in_=weights[w].rearrange("(p t) n -> p t n", t=4))
 
         def load_thrust(r0, r1, buffer=None):
-            raw = keep.tile([P, r1 - r0, T], BF16, name=buffer or "raw_thrust%d" % r0, align_bytes=256)
+            raw = keep.tile([P, r1 - r0, T], BF16, name=buffer or "raw_thrust%d" % r0, align_bytes=ALIGN)
             nc.sync.dma_start(out=raw[:], in_=thrust_rows[:, r0:r1, :])
             for r in range(r0, r1):
                 thrust_raw[r] = raw[:, r - r0, :]
 
         def load_outer(r0, r1, buffer=None):
-            raw = keep.tile([P, r1 - r0, L], BF16, name=buffer or "raw_outer%d" % r0, align_bytes=256)
+            raw = keep.tile([P, r1 - r0, L], BF16, name=buffer or "raw_outer%d" % r0, align_bytes=ALIGN)
             nc.sync.dma_start(out=raw[:], in_=outer_rows[:, r0:r1, :])
             for r in range(r0, r1):
                 outer_raw[r] = raw[:, r - r0, :]
 
-        w_codes = [keep.tile([P, N], U32, name="w_codes_%d" % w, align_bytes=256) for w in range(PASSES)]
-        w_scales = [keep.tile([P, N], U8, name="w_scales_%d" % w, align_bytes=256) for w in range(PASSES)]
+        w_codes = [keep.tile([P, N], U32, name="w_codes_%d" % w, align_bytes=ALIGN) for w in range(PASSES)]
+        w_scales = [keep.tile([P, N], U8, name="w_scales_%d" % w, align_bytes=ALIGN) for w in range(PASSES)]
         w_laid = {}
 
         def lay_weights(w, c0, c1, copy):
             if w not in w_laid:
-                w_laid[w] = keep.tile([P, N, 4], BF16, name="laid_w%d" % w, align_bytes=256)
+                w_laid[w] = keep.tile([P, N, 4], BF16, name="laid_w%d" % w, align_bytes=ALIGN)
             copy(
-                out=w_laid[w][:, c0:c1].rearrange("p (c i) t -> p c t i", i=8),
-                in_=w_raw[w][:, :, c0:c1].rearrange("p t (c i) -> p c t i", i=8),
+                out=w_laid[w][:, c0:c1].rearrange("p (c i) t -> p c t i", i=LINE),
+                in_=w_raw[w][:, :, c0:c1].rearrange("p t (c i) -> p c t i", i=LINE),
             )
 
         def lay_weights_both(w):
@@ -99,10 +102,10 @@ def tile_wind_farm_wakes_s2_kernel(tc, thrust, area, kern, outer, okern, inflow,
                 in_=w_laid[w][:, c0:c1].rearrange("p c t -> p (c t)"),
             )
 
-        a_codes = keep.tile([P, STAGGER + TILES * T_PASSES * P], U32, name="a_codes", align_bytes=256)[:, STAGGER:]
-        a_scales = keep.tile([P, TILES * T_PASSES * P], U8, name="a_scales", align_bytes=256)
-        o_codes = keep.tile([P, STAGGER + TILES * L_PASSES * P], U32, name="o_codes", align_bytes=256)[:, STAGGER:]
-        o_scales = keep.tile([P, TILES * L_PASSES * P], U8, name="o_scales", align_bytes=256)
+        a_codes = keep.tile([P, STAGGER + TILES * T_PASSES * P], U32, name="a_codes", align_bytes=ALIGN)[:, STAGGER:]
+        a_scales = keep.tile([P, TILES * T_PASSES * P], U8, name="a_scales", align_bytes=ALIGN)
+        o_codes = keep.tile([P, STAGGER + TILES * L_PASSES * P], U32, name="o_codes", align_bytes=ALIGN)[:, STAGGER:]
+        o_scales = keep.tile([P, TILES * L_PASSES * P], U8, name="o_scales", align_bytes=ALIGN)
 
         banks = {}
         held = {}
@@ -129,13 +132,13 @@ def tile_wind_farm_wakes_s2_kernel(tc, thrust, area, kern, outer, okern, inflow,
         def turn_outer(b):
             turn(("outer", b), [(outer_raw[s // L_PASSES], s % L_PASSES) for s in (2 * b, 2 * b + 1)])
 
-        area_rows = keep.tile([P, T_PASSES, P, 4], BF16, name="area_rows", align_bytes=256)
+        area_rows = keep.tile([P, T_PASSES, P, 4], BF16, name="area_rows", align_bytes=ALIGN)
         thrust_sq = {}
         a_pair = {}
-        outer_laid = keep.tile([P, OUTER_BANKS, 2 * P, 2], F32, name="outer_laid", align_bytes=256)
+        outer_laid = keep.tile([P, OUTER_BANKS, 2 * P, 2], F32, name="outer_laid", align_bytes=ALIGN)
 
         def square_thrust(r):
-            thrust_sq[r] = work.tile([P, 2 * P, 4], F32, name="square", bufs=SQUARES, align_bytes=256)
+            thrust_sq[r] = work.tile([P, 2 * P, 4], F32, name="square", bufs=SQUARES, align_bytes=ALIGN)
             nc.scalar.activation(
                 out=thrust_sq[r][:].rearrange("p c (u e) -> p c u e", e=2),
                 in_=banks["thrust", r][:].bitcast(BF16).rearrange("p u (c e) -> p c u e", e=2),
@@ -145,7 +148,7 @@ def tile_wind_farm_wakes_s2_kernel(tc, thrust, area, kern, outer, okern, inflow,
 
         def times_area(r):
             if r % 2 == 0:
-                a_pair[r // 2] = work.tile([P, 2, T_PASSES, P, 4], BF16, name="a_pair", bufs=2, align_bytes=256)
+                a_pair[r // 2] = work.tile([P, 2, T_PASSES, P, 4], BF16, name="a_pair", align_bytes=ALIGN)
             nc.vector.tensor_tensor(
                 out=a_pair[r // 2][:, r % 2],
                 in0=thrust_sq[r][:].rearrange("p (g c) t -> p g c t", g=T_PASSES),
@@ -154,10 +157,10 @@ def tile_wind_farm_wakes_s2_kernel(tc, thrust, area, kern, outer, okern, inflow,
             )
 
         def quantise_a(r0, r1):
-            cols = slice(r0 * T_PASSES * P, r1 * T_PASSES * P)
+            part = slice(r0 * T_PASSES * P, r1 * T_PASSES * P)
             nc.vector.quantize_mx(
-                out=a_codes[:, cols].bitcast(E5M2),
-                scales=a_scales[:, cols],
+                out=a_codes[:, part].bitcast(E5M2),
+                scales=a_scales[:, part],
                 in_=a_pair[r0 // 2][:, r0 % 2:r0 % 2 + r1 - r0].rearrange("p r g c t -> p (r g c t)"),
             )
 
@@ -166,9 +169,9 @@ def tile_wind_farm_wakes_s2_kernel(tc, thrust, area, kern, outer, okern, inflow,
             give_bank(("outer", b))
 
         def quantise_outer(b0, b1):
-            cols = slice(b0 * 2 * P, b1 * 2 * P)
+            part = slice(b0 * 2 * P, b1 * 2 * P)
             values = outer_laid[:, b0:b1].rearrange("p b c u -> p (b c u)").bitcast(BF16)
-            nc.vector.quantize_mx(out=o_codes[:, cols].bitcast(E4M3), scales=o_scales[:, cols], in_=values)
+            nc.vector.quantize_mx(out=o_codes[:, part].bitcast(E4M3), scales=o_scales[:, part], in_=values)
 
         def add_passes(r, h, passes):
             if (r, h) not in banks:
@@ -177,11 +180,11 @@ def tile_wind_farm_wakes_s2_kernel(tc, thrust, area, kern, outer, okern, inflow,
             order = KERN + OKERN if r < OKERN_FIRST_FROM else OKERN + KERN
             for w in passes:
                 if w in KERN:
-                    rows = slice((r * T_PASSES + w) * P, (r * T_PASSES + w + 1) * P)
-                    codes, scales = a_codes[:, rows].bitcast(E5M2), a_scales[:, rows]
+                    part = slice((r * T_PASSES + w) * P, (r * T_PASSES + w + 1) * P)
+                    codes, scales = a_codes[:, part].bitcast(E5M2), a_scales[:, part]
                 else:
-                    rows = slice((r * L_PASSES + w - T_PASSES) * P, (r * L_PASSES + w - T_PASSES + 1) * P)
-                    codes, scales = o_codes[:, rows].bitcast(E4M3), o_scales[:, rows]
+                    part = slice((r * L_PASSES + w - T_PASSES) * P, (r * L_PASSES + w - T_PASSES + 1) * P)
+                    codes, scales = o_codes[:, part].bitcast(E4M3), o_scales[:, part]
                 nc.tensor.matmul_mx(
                     out=banks[r, h][:],
                     lhsT=codes,
@@ -210,7 +213,7 @@ def tile_wind_farm_wakes_s2_kernel(tc, thrust, area, kern, outer, okern, inflow,
             if second_half:
                 return second_half.pop()
             name = RESULT_BUFFERS[(len(speed_sb) + len(power_sb)) // 2]
-            both = keep.tile([P, 2, N], F32, name=name, align_bytes=256)
+            both = keep.tile([P, 2, N], F32, name=name, align_bytes=ALIGN)
             second_half.append(both[:, 1, :])
             return both[:, 0, :]
 
@@ -226,7 +229,7 @@ def tile_wind_farm_wakes_s2_kernel(tc, thrust, area, kern, outer, okern, inflow,
 
         def square_speed(r, c0=0, c1=N):
             if r not in speed_sq:
-                speed_sq[r] = work.tile([P, N], F32, name="square", bufs=SQUARES, align_bytes=256)
+                speed_sq[r] = work.tile([P, N], F32, name="square", bufs=SQUARES, align_bytes=ALIGN)
             nc.scalar.activation(
                 out=speed_sq[r][:, c0:c1], in_=root[r][:, c0:c1], func=ACT.Square, scale=-1.0, bias=inflow_m[:, r:r + 1]
             )
@@ -234,10 +237,10 @@ def tile_wind_farm_wakes_s2_kernel(tc, thrust, area, kern, outer, okern, inflow,
         def store_speed(r):
             speed_sb[r] = result_tile()
             nc.vector.tensor_scalar(
-                out=speed_sb[r][:, 0:N], in0=root[r][:, 0:N], scalar1=-1.0, scalar2=inflow_m[:, r:r + 1],
+                out=speed_sb[r], in0=root[r][:], scalar1=-1.0, scalar2=inflow_m[:, r:r + 1],
                 op0=ALU.mult, op1=ALU.add,
             )
-            nc.sync.dma_start(out=speed_rows[:, r, 0:N], in_=speed_sb[r][:, 0:N])
+            nc.sync.dma_start(out=speed_rows[:, r, :], in_=speed_sb[r])
 
         def store_power(r, c0=0, c1=N):
             if r not in power_sb:
@@ -247,8 +250,8 @@ def tile_wind_farm_wakes_s2_kernel(tc, thrust, area, kern, outer, okern, inflow,
             )
             nc.sync.dma_start(out=power_rows[:, r, c0:c1], in_=power_sb[r][:, c0:c1])
 
-        nc.scalar.dma_start(out=area_k[:], in_=area.rearrange("(g p t) -> p g t", g=T_PASSES, t=4))
         nc.scalar.activation(out=warm[:], in_=warm[:], func=ACT.Sqrt)
+        nc.scalar.dma_start(out=area_k[:], in_=area.rearrange("(g p t) -> p g t", g=T_PASSES, t=4))
 
         load_thrust(0, 1)
         load_thrust(1, 2)

@@ -48,9 +48,10 @@ def tile_wind_farm_wakes_s2_kernel(tc, thrust, area, kern, outer, okern, inflow,
         area_k = keep.tile([P, T_PASSES, 4], BF16, name="area_k")
         inflow_m = keep.tile([P, TILES], BF16, name="inflow_m")
         warm = keep.tile([P, 1], F32, name="warm")
-        nc.gpsimd.memset(warm[:], 1.0)
+        nc.vector.memset(warm[:], 1.0)
         ident = keep.tile([P, P], F32, name="ident")
-        make_identity(nc, ident[:])
+        nc.vector.memset(ident[:], 0.0)
+        make_identity(nc, ident[:], nomemset=True)
 
         weights = [kern[g * PASS:(g + 1) * PASS, :] for g in range(T_PASSES)]
         weights = weights + [okern[g * PASS:(g + 1) * PASS, :] for g in range(L_PASSES)]
@@ -138,10 +139,10 @@ def tile_wind_farm_wakes_s2_kernel(tc, thrust, area, kern, outer, okern, inflow,
         outer_laid = keep.tile([P, OUTER_BANKS, 2 * P, 2], F32, name="outer_laid", align_bytes=ALIGN)
 
         def square_thrust(r):
-            thrust_sq[r] = work.tile([P, 2 * P, 4], F32, name="square", bufs=SQUARES, align_bytes=ALIGN)
+            thrust_sq[r] = work.tile([P, 2, 2 * P, 2], F32, name="square", bufs=SQUARES, align_bytes=ALIGN)
             nc.scalar.activation(
-                out=thrust_sq[r][:].rearrange("p c (u e) -> p c u e", e=2),
-                in_=banks["thrust", r][:].bitcast(BF16).rearrange("p u (c e) -> p c u e", e=2),
+                out=thrust_sq[r][:].rearrange("p u c e -> p (u c e)"),
+                in_=banks["thrust", r][:].bitcast(BF16).rearrange("p u c -> p (u c)"),
                 func=ACT.Square,
             )
             give_bank(("thrust", r))
@@ -150,9 +151,9 @@ def tile_wind_farm_wakes_s2_kernel(tc, thrust, area, kern, outer, okern, inflow,
             if r % 2 == 0:
                 a_pair[r // 2] = work.tile([P, 2, T_PASSES, P, 4], BF16, name="a_pair", align_bytes=ALIGN)
             nc.vector.tensor_tensor(
-                out=a_pair[r // 2][:, r % 2],
-                in0=thrust_sq[r][:].rearrange("p (g c) t -> p g c t", g=T_PASSES),
-                in1=area_rows[:],
+                out=a_pair[r // 2][:, r % 2].rearrange("p g c (u e) -> p (g c) u e", e=2),
+                in0=thrust_sq[r][:].rearrange("p u c e -> p c u e"),
+                in1=area_rows[:].rearrange("p g c (u e) -> p (g c) u e", e=2),
                 op=ALU.mult,
             )
 

from contextlib import ExitStack

import concourse.mybir as mybir
from concourse.masks import make_identity

M, T, L, N = 1024, 1024, 1536, 1024
FLOPS = 2 * M * N * (T + L)

F32 = mybir.dt.float32
BF16 = mybir.dt.bfloat16
U32 = mybir.dt.uint32
U8 = mybir.dt.uint8
E4M3 = mybir.dt.float8_e4m3fn_x4
E5M2 = mybir.dt.float8_e5m2_x4
ACT = mybir.ActivationFunctionType
ALU = mybir.AluOpType

P = 128
PASS = 512
T_PASSES = T // PASS
L_PASSES = L // PASS
PASSES = T_PASSES + L_PASSES
KERN = list(range(T_PASSES))
OKERN = list(range(T_PASSES, PASSES))
TILES = M // P
HALF = 512
BANKS = 8
OUTER_BANKS = TILES * L_PASSES // 2
VECTOR_COLUMNS = [608, 640, 512, 512, 640]
OKERN_FIRST_FROM = 4
ALIGN = 256
STAGGER = 32
LINE = 8
SQUARES = 6
ROOTS = 4
A_PAIRS = 2
RESULT_BUFFERS = ["laid_w0", "laid_w1", "raw_w2", "raw_w3", "raw_w4", "laid_w2", "laid_w3", "laid_w4"]


def tile_wind_farm_wakes_s2_kernel(tc, thrust, area, kern, outer, okern, inflow, speed, power):
    nc = tc.nc
    with ExitStack() as ctx:
        keep = ctx.enter_context(tc.tile_pool(name="keep", bufs=1))
        work = ctx.enter_context(tc.tile_pool(name="work", bufs=A_PAIRS))
        psum = ctx.enter_context(tc.psum_pool(name="psum", bufs=1))
        ctx.enter_context(tc.manual_schedule())

        area_k = keep.tile([P, T_PASSES, 4], BF16, name="area_k")
        inflow_m = keep.tile([P, TILES], BF16, name="inflow_m")
        warm = keep.tile([P, 1], F32, name="warm")
        nc.vector.memset(warm[:], 1.0)
        ident = keep.tile([P, P], F32, name="ident")
        nc.vector.memset(ident[:], 0.0)
        make_identity(nc, ident[:], nomemset=True)

        weights = [kern[g * PASS:(g + 1) * PASS, :] for g in range(T_PASSES)]
        weights = weights + [okern[g * PASS:(g + 1) * PASS, :] for g in range(L_PASSES)]
        thrust_rows = thrust.rearrange("(p r) k -> p r k", r=TILES)
        outer_rows = outer.rearrange("(p r) k -> p r k", r=TILES)
        speed_rows = speed.rearrange("(p r) n -> p r n", r=TILES)
        power_rows = power.rearrange("(p r) n -> p r n", r=TILES)

        w_raw = {}
        thrust_raw = {}
        outer_raw = {}

        def load_weights(w):
            w_raw[w] = keep.tile([P, 4, N], BF16, name="raw_w%d" % w, align_bytes=ALIGN)
            nc.sync.dma_start(out=w_raw[w][:], in_=weights[w].rearrange("(p t) n -> p t n", t=4))

        def load_thrust(r0, r1, buffer=None):
            raw = keep.tile([P, r1 - r0, T], BF16, name=buffer or "raw_thrust%d" % r0, align_bytes=ALIGN)
            nc.sync.dma_start(out=raw[:], in_=thrust_rows[:, r0:r1, :])
            for r in range(r0, r1):
                thrust_raw[r] = raw[:, r - r0, :]

        def load_outer(r0, r1, buffer=None):
            raw = keep.tile([P, r1 - r0, L], BF16, name=buffer or "raw_outer%d" % r0, align_bytes=ALIGN)
            nc.sync.dma_start(out=raw[:], in_=outer_rows[:, r0:r1, :])
            for r in range(r0, r1):
                outer_raw[r] = raw[:, r - r0, :]

        w_codes = [keep.tile([P, N], U32, name="w_codes_%d" % w, align_bytes=ALIGN) for w in range(PASSES)]
        w_scales = [keep.tile([P, N], U8, name="w_scales_%d" % w, align_bytes=ALIGN) for w in range(PASSES)]
        w_laid = {}

        def lay_weights(w, c0, c1, copy):
            if w not in w_laid:
                w_laid[w] = keep.tile([P, N, 4], BF16, name="laid_w%d" % w, align_bytes=ALIGN)
            copy(
                out=w_laid[w][:, c0:c1].rearrange("p (c i) t -> p c t i", i=LINE),
                in_=w_raw[w][:, :, c0:c1].rearrange("p t (c i) -> p c t i", i=LINE),
            )

        def lay_weights_both(w):
            lay_weights(w, 0, VECTOR_COLUMNS[w], nc.vector.tensor_copy)
            lay_weights(w, VECTOR_COLUMNS[w], N, nc.scalar.copy)

        def quantise_weights(w, c0, c1):
            nc.vector.quantize_mx(
                out=w_codes[w][:, c0:c1].bitcast(E4M3),
                scales=w_scales[w][:, c0:c1],
                in_=w_laid[w][:, c0:c1].rearrange("p c t -> p (c t)"),
            )

        a_codes = keep.tile([P, STAGGER + TILES * T_PASSES * P], U32, name="a_codes", align_bytes=ALIGN)[:, STAGGER:]
        a_scales = keep.tile([P, TILES * T_PASSES * P], U8, name="a_scales", align_bytes=ALIGN)
        o_codes = keep.tile([P, STAGGER + TILES * L_PASSES * P], U32, name="o_codes", align_bytes=ALIGN)[:, STAGGER:]
        o_scales = keep.tile([P, TILES * L_PASSES * P], U8, name="o_scales", align_bytes=ALIGN)

        banks = {}
        held = {}
        empty = list(range(BANKS))

        def take_bank(key, shape):
            held[key] = empty.pop(0)
            banks[key] = psum.tile(shape, F32, name="bank_%d" % held[key])
            return banks[key]

        def give_bank(key):
            empty.append(held.pop(key))

        def turn(key, units):
            bank = take_bank(key, [P, 2, 2 * P])
            for s, (raw, g) in enumerate(units):
                words = raw.bitcast(F32)
                for u in range(2):
                    nc.tensor.transpose(bank[:, u, s * P:(s + 1) * P], words[:, 256 * g + u:256 * (g + 1):2], ident[:])

        def turn_thrust(r):
            turn(("thrust", r), [(thrust_raw[r], g) for g in range(T_PASSES)])

        def turn_outer(b):
            turn(("outer", b), [(outer_raw[s // L_PASSES], s % L_PASSES) for s in (2 * b, 2 * b + 1)])

        area_rows = keep.tile([P, T_PASSES, P, 4], BF16, name="area_rows", align_bytes=ALIGN)
        thrust_sq = {}
        a_pair = {}
        outer_laid = keep.tile([P, OUTER_BANKS, 2 * P, 2], F32, name="outer_laid", align_bytes=ALIGN)

        def square_thrust(r):
            thrust_sq[r] = work.tile([P, 2, 2 * P, 2], F32, name="square", bufs=SQUARES, align_bytes=ALIGN)
            nc.scalar.activation(
                out=thrust_sq[r][:].rearrange("p u c e -> p (u c e)"),
                in_=banks["thrust", r][:].bitcast(BF16).rearrange("p u c -> p (u c)"),
                func=ACT.Square,
            )
            give_bank(("thrust", r))

        def times_area(r):
            if r % 2 == 0:
                a_pair[r // 2] = work.tile([P, 2, T_PASSES, P, 4], BF16, name="a_pair", align_bytes=ALIGN)
            nc.vector.tensor_tensor(
                out=a_pair[r // 2][:, r % 2].rearrange("p g c (u e) -> p (g c) u e", e=2),
                in0=thrust_sq[r][:].rearrange("p u c e -> p c u e"),
                in1=area_rows[:].rearrange("p g c (u e) -> p (g c) u e", e=2),
                op=ALU.mult,
            )

        def quantise_a(r0, r1):
            part = slice(r0 * T_PASSES * P, r1 * T_PASSES * P)
            nc.vector.quantize_mx(
                out=a_codes[:, part].bitcast(E5M2),
                scales=a_scales[:, part],
                in_=a_pair[r0 // 2][:, r0 % 2:r0 % 2 + r1 - r0].rearrange("p r g c t -> p (r g c t)"),
            )

        def lay_outer(b, copy=nc.scalar.copy):
            copy(out=outer_laid[:, b], in_=banks["outer", b][:].rearrange("p u c -> p c u"))
            give_bank(("outer", b))

        def quantise_outer(b0, b1):
            part = slice(b0 * 2 * P, b1 * 2 * P)
            values = outer_laid[:, b0:b1].rearrange("p b c u -> p (b c u)").bitcast(BF16)
            nc.vector.quantize_mx(out=o_codes[:, part].bitcast(E4M3), scales=o_scales[:, part], in_=values)

        def add_passes(r, h, passes):
            if (r, h) not in banks:
                take_bank((r, h), [P, HALF])
            cols = slice(h * HALF, (h + 1) * HALF)
            order = KERN + OKERN if r < OKERN_FIRST_FROM else OKERN + KERN
            for w in passes:
                if w in KERN:
                    part = slice((r * T_PASSES + w) * P, (r * T_PASSES + w + 1) * P)
                    codes, scales = a_codes[:, part].bitcast(E5M2), a_scales[:, part]
                else:
                    part = slice((r * L_PASSES + w - T_PASSES) * P, (r * L_PASSES + w - T_PASSES + 1) * P)
                    codes, scales = o_codes[:, part].bitcast(E4M3), o_scales[:, part]
                nc.tensor.matmul_mx(
                    out=banks[r, h][:],
                    lhsT=codes,
                    lhsT_scale=scales,
                    rhs=w_codes[w][:, cols].bitcast(E4M3),
                    rhs_scale=w_scales[w][:, cols],
                    start=(w == order[0]),
                    stop=(w == order[-1]),
                )

        def add_pass_to_tiles(w, h, tiles):
            for r in tiles:
                add_passes(r, h, [w])

        def add_to_tile(r, passes):
            for h in range(2):
                add_passes(r, h, passes)

        root = {}
        speed_sb = {}
        speed_sq = {}
        power_sb = {}
        second_half = []

        def result_tile():
            if second_half:
                return second_half.pop()
            name = RESULT_BUFFERS[(len(speed_sb) + len(power_sb)) // 2]
            both = keep.tile([P, 2, N], F32, name=name, align_bytes=ALIGN)
            second_half.append(both[:, 1, :])
            return both[:, 0, :]

        def take_root(r, h):
            if r not in root:
                root[r] = work.tile([P, N], F32, name="root", bufs=ROOTS)
            nc.scalar.activation(out=root[r][:, h * HALF:(h + 1) * HALF], in_=banks[r, h][:], func=ACT.Sqrt)
            give_bank((r, h))

        def take_roots(r):
            for h in range(2):
                take_root(r, h)

        def square_speed(r, c0=0, c1=N):
            if r not in speed_sq:
                speed_sq[r] = work.tile([P, N], F32, name="square", bufs=SQUARES, align_bytes=ALIGN)
            nc.scalar.activation(
                out=speed_sq[r][:, c0:c1], in_=root[r][:, c0:c1], func=ACT.Square, scale=-1.0, bias=inflow_m[:, r:r + 1]
            )

        def store_speed(r):
            speed_sb[r] = result_tile()
            nc.vector.tensor_scalar(
                out=speed_sb[r], in0=root[r][:], scalar1=-1.0, scalar2=inflow_m[:, r:r + 1],
                op0=ALU.mult, op1=ALU.add,
            )
            nc.sync.dma_start(out=speed_rows[:, r, :], in_=speed_sb[r])

        def store_power(r, c0=0, c1=N):
            if r not in power_sb:
                power_sb[r] = result_tile()
            nc.vector.tensor_tensor(
                out=power_sb[r][:, c0:c1], in0=speed_sq[r][:, c0:c1], in1=speed_sb[r][:, c0:c1], op=ALU.mult
            )
            nc.sync.dma_start(out=power_rows[:, r, c0:c1], in_=power_sb[r][:, c0:c1])

        nc.scalar.activation(out=warm[:], in_=warm[:], func=ACT.Sqrt)
        nc.scalar.dma_start(out=area_k[:], in_=area.rearrange("(g p t) -> p g t", g=T_PASSES, t=4))

        load_thrust(0, 1)
        load_thrust(1, 2)
        load_thrust(2, 4)
        load_weights(0)
        load_thrust(4, 6)
        load_outer(0, 2)
        load_weights(1)
        load_outer(2, 4)
        for w in OKERN:
            load_weights(w)
        load_outer(4, 5, "raw_thrust2")
        load_outer(5, 6, "raw_thrust4")
        nc.sync.dma_start(out=inflow_m[:], in_=inflow.rearrange("(p r) -> p r", r=TILES))

        nc.vector.tensor_copy(out=area_rows[:], in_=area_k[:].unsqueeze(2).to_broadcast([P, T_PASSES, P, 4]))
        for r in range(4):
            turn_thrust(r)
        square_thrust(0)
        square_thrust(1)
        times_area(0)
        square_thrust(2)
        times_area(1)
        square_thrust(3)
        lay_weights(0, 0, VECTOR_COLUMNS[0], nc.vector.tensor_copy)
        quantise_a(0, 2)
        lay_weights(0, VECTOR_COLUMNS[0], N, nc.scalar.copy)
        load_thrust(6, 8, "raw_w0")
        turn_thrust(4)
        turn_thrust(5)
        times_area(2)
        square_thrust(4)
        quantise_weights(0, 0, HALF)
        times_area(3)
        quantise_weights(0, HALF, N)
        square_thrust(5)

        for b in range(0, 3):
            turn_outer(b)
        for h in range(2):
            add_pass_to_tiles(0, h, [0, 1])
        quantise_a(2, 4)
        for b in range(0, 3):
            lay_outer(b)
        lay_weights_both(1)
        load_outer(6, 8, "raw_w1")
        quantise_outer(0, 2)
        quantise_weights(1, 0, HALF)
        for b in range(3, 6):
            turn_outer(b)
        add_pass_to_tiles(1, 0, [0, 1])
        quantise_outer(2, 3)
        quantise_weights(1, HALF, N)
        add_pass_to_tiles(1, 1, [0, 1])
        for b in range(3, 6):
            lay_outer(b)
        add_to_tile(2, KERN)

        early = [0, 1, 2]
        lay_weights_both(2)
        quantise_outer(3, 5)
        quantise_weights(2, 0, HALF)
        add_pass_to_tiles(2, 0, early)
        lay_weights_both(3)
        quantise_weights(2, HALF, N)
        quantise_weights(3, 0, HALF)
        add_pass_to_tiles(2, 1, early)
        add_pass_to_tiles(3, 0, early)
        lay_weights_both(4)
        turn_outer(6)
        turn_outer(7)
        quantise_weights(3, HALF, N)
        quantise_weights(4, 0, HALF)
        add_pass_to_tiles(3, 1, [0, 1])
        add_pass_to_tiles(4, 0, early)
        quantise_outer(5, 6)
        lay_outer(6)
        lay_outer(7)
        quantise_weights(4, HALF, N)
        add_pass_to_tiles(4, 1, [0, 1])
        add_passes(2, 1, [3, 4])

        times_area(4)
        take_root(0, 0)
        take_root(1, 0)
        turn_outer(8)
        take_root(0, 1)
        add_to_tile(3, KERN + OKERN)
        quantise_outer(6, 8)
        quantise_a(4, 5)
        take_root(1, 1)
        store_speed(0)
        square_speed(0)
        store_speed(1)
        times_area(5)
        square_speed(1)
        add_passes(4, 0, OKERN + KERN)

        take_roots(2)
        store_power(0)
        quantise_a(5, 6)
        lay_outer(8)
        turn_thrust(6)
        turn_outer(10)
        add_passes(4, 1, OKERN + KERN)
        turn_outer(9)
        store_power(1)
        store_speed(2)
        quantise_outer(8, 9)
        square_speed(2)
        store_power(2)

        take_roots(3)
        turn_outer(11)
        turn_thrust(7)
        store_speed(3)
        lay_outer(10, nc.vector.tensor_copy)
        lay_outer(9, nc.vector.tensor_copy)
        add_to_tile(5, OKERN + KERN)
        square_thrust(6)
        square_speed(3)
        times_area(6)
        quantise_outer(9, 11)
        store_power(3)
        add_to_tile(6, OKERN)

        take_roots(4)
        store_speed(4)
        quantise_a(6, 7)
        add_to_tile(6, KERN)
        lay_outer(11)
        square_speed(4)
        square_thrust(7)
        store_power(4)
        quantise_outer(11, 12)
        add_to_tile(7, OKERN)
        times_area(7)

        take_roots(5)
        store_speed(5)
        quantise_a(7, 8)
        add_to_tile(7, KERN)
        take_roots(6)
        square_speed(5)
        store_speed(6)
        store_power(5)
        square_speed(6)
        store_power(6)

        take_roots(7)
        store_speed(7)
        for h in range(2):
            square_speed(7, h * HALF, (h + 1) * HALF)
        for h in range(2):
            store_power(7, h * HALF, (h + 1) * HALF)
